import numpy as np
import ml_dtypes


def mxq(x, axis, fmt="e4m3"):
    dtype, down = {"e4m3": (ml_dtypes.float8_e4m3fn, 7), "e5m2": (ml_dtypes.float8_e5m2, 14)}[fmt]
    v = np.moveaxis(np.asarray(x, np.float32).astype(ml_dtypes.bfloat16).astype(np.float64), axis, -1)
    blocks = v.reshape(v.shape[:-1] + (-1, 32))
    amax = np.abs(blocks).max(-1, keepdims=True)
    byte = np.maximum(np.where(amax > 0, np.frexp(amax)[1] - 1 + 127, 0) - down, 1)
    scale = np.exp2(byte - 127.0)
    codes = (blocks / scale).astype(np.float32).astype(dtype).astype(np.float64)
    return np.moveaxis((codes * scale).reshape(v.shape), -1, axis)


WIDE = False


def mx_kscale(k):
    if not WIDE:
        return np.ones(k)
    levels = np.array([10, -10, 5, -5, 0])
    if k % 512:
        return np.exp2(np.random.permutation(np.resize(levels, k // 32))).repeat(32)
    a = np.empty((k // 512, 16))
    for p in range(k // 512):
        a[p, :8] = np.random.permutation(np.resize(levels, 8))
        for g in range(8):
            far = levels[np.abs(levels - a[p, g]) >= 10]
            a[p, g + 8] = far[np.random.randint(len(far))]
    return np.exp2(a.ravel()).repeat(32)


def f64(x):
    return np.asarray(x).astype(np.float64)


def striped(idx):
    return np.tile(idx.reshape(-1, 16).T, (8, 1)).astype(np.uint16)


def unstriped(offs):
    return offs[:16].T.reshape(-1).astype(np.int64)


def pack_weight(w):
    k, n = w.shape
    w = f64(np.asarray(w, np.float32).astype(ml_dtypes.bfloat16)).reshape(k // 32, 32, n)
    amax = np.abs(w).max(1)
    byte = np.clip(np.where(amax > 0, np.frexp(amax)[1] - 1 + 127 - 7, 1), 1, 254)
    scaled = (w * np.exp2(127.0 - byte)[:, None, :]).reshape(k, n).astype(np.float32)
    words = np.ascontiguousarray(scaled.reshape(k // 512, 128, 4, n).transpose(0, 1, 3, 2)).astype(ml_dtypes.float8_e4m3fn).view(np.uint8)
    return words, np.ascontiguousarray(byte.astype(np.uint8).reshape(k // 512, 16, n))


def unpack_weight(words, scales):
    g, p, n, _ = words.shape
    vals = np.ascontiguousarray(words).view(ml_dtypes.float8_e4m3fn).astype(np.float64) * np.repeat(np.exp2(scales.astype(np.float64) - 127.0), 8, axis=1)[..., None]
    return vals.transpose(0, 1, 3, 2).reshape(g * 512, n)


def planes(y):
    n, m = y.shape
    v = y.astype(np.float32).astype(ml_dtypes.bfloat16).astype(np.float64).reshape(n // 32, 32, m)
    top = np.abs(v).max(1)
    byte = np.clip(np.where(top > 0, np.frexp(top)[1] - 1 + 127 - 7, 1), 1, 254)
    codes = (v * np.exp2(127.0 - byte)[:, None, :]).reshape(n, m).astype(np.float32).astype(ml_dtypes.float8_e4m3fn).view(np.uint8)
    words = codes.reshape(n // 512, 128, 4, m).transpose(0, 1, 3, 2)
    return np.ascontiguousarray(words), np.ascontiguousarray(byte.astype(np.uint8).reshape(n // 512, 16, m))


def relu(v):
    return np.maximum(v, 0.0)


K, T, S, D, N = 1024, 1024, 512, 2, 512
P = 2 ** 7


def setup_inputs():
    n = np.random.standard_normal
    s = mx_kscale(K)[:, None]
    packed_xT = pack_weight(n((K, T)) * s)
    return {
        "x_words": packed_xT[0],
        "x_scales": packed_xT[1],
        "w1": (n((K, N)) / np.sqrt(K) / s).astype(np.float32),
        "w2": (n((K, N)) / np.sqrt(K) / s).astype(np.float32),
        "gate": (np.tile(np.random.dirichlet(np.ones(D), T).T[:, None, :], (1, P, 1))).astype(np.float32),
        "offs": striped(np.random.permutation(T)[:S]),
    }


def reference(x_words, x_scales, w1, w2, gate, offs):
    xq = unpack_weight(x_words, x_scales)[:, unstriped(offs)]
    g0 = f64(gate)[0, :1][:, unstriped(offs)]
    g1 = f64(gate)[1, :1][:, unstriped(offs)]
    out_0 = (relu(mxq(f64(w1), 0, "e4m3").T @ xq)) * g0 + (relu(mxq(f64(w2), 0, "e4m3").T @ xq)) * g1
    return (out_0,) + planes(out_0)

@@ -1,0 +1,224 @@
+from contextlib import ExitStack
+
+import concourse.mybir as mybir
+from concourse.masks import make_identity
+
+K, T, S, N = 1024, 1024, 512, 512
+P = 128
+PACK = 4
+PASSES = K // (P * PACK)
+HALF = N // 2
+BLOCKS = S // P
+
+FLOPS = 2 * 2 * K * N * S
+BYTES = 2 * K * N * 4 + K * T + K * T // 32 + 2 * T * 4 + P * (S // 16) * 2 + N * S * 4 + N * S + N * S // 32
+
+F32 = mybir.dt.float32
+BF16 = mybir.dt.bfloat16
+I32 = mybir.dt.int32
+U32 = mybir.dt.uint32
+U16 = mybir.dt.uint16
+U8 = mybir.dt.uint8
+FP8X4 = mybir.dt.float8_e4m3fn_x4
+MAX = mybir.AluOpType.max
+MULT = mybir.AluOpType.mult
+
+VECTOR_COLUMNS = (128, 0, 128, 0, 160, 96, 0, 256)
+SCALAR_GATED = ((1, 0, 0),)
+Y_COPY = "VSSS"
+Y_ROUND = "VVVV"
+QUANTIZE_FIRST = (False, False, True)
+RELU = mybir.ActivationFunctionType.Relu
+COPY = mybir.ActivationFunctionType.Copy
+
+
+def tile_picked_zsmoe_relu_po_kernel(
+    tc, x_words, x_scales, w1, w2, gate, offs, out_0, out_1, out_2
+):
+    nc = tc.nc
+    weights = (w1, w2)
+    pieces = [(d, h, a) for d in range(2) for h in range(2) for a in range(PASSES)]
+
+    with ExitStack() as ctx:
+        keep = ctx.enter_context(tc.tile_pool(name="keep", bufs=1))
+        psum = ctx.enter_context(tc.psum_pool(name="psum", bufs=1))
+
+        offsets = keep.tile([P, S // 16], U16, name="offsets")
+        word_table = [keep.tile([P, T], U32, name="word_table%d" % a, align_bytes=64) for a in range(PASSES)]
+        scale_table = keep.tile([P, T], U8, name="scale_table", align_bytes=64)
+        gate_table = keep.tile([P, T], F32, name="gate_table", align_bytes=64)
+        raw = {q: keep.tile([P, PACK, HALF], F32, name="raw%d%d%d" % q, align_bytes=64) for q in pieces}
+        rounded = {q: keep.tile([P, HALF, PACK], BF16, name="rounded%d%d%d" % q, align_bytes=64) for q in pieces}
+        w_words = {q: keep.tile([P, HALF], U32, name="w_words%d%d%d" % q, align_bytes=64) for q in pieces}
+        w_scales = {q: keep.tile([P, HALF], U8, name="w_scales%d%d%d" % q, align_bytes=64) for q in pieces}
+        picked_words = [keep.tile([P, S], U32, name="picked_words%d" % a, align_bytes=64) for a in range(PASSES)]
+        picked_scales = keep.tile([P, S], U8, name="picked_scales", align_bytes=64)
+        picked_gate = keep.tile([P, S], F32, name="picked_gate", align_bytes=64)
+        token_gate = keep.tile([P, BLOCKS, 2], F32, name="token_gate", align_bytes=64)
+        identity = keep.tile([P, P], F32, name="identity", align_bytes=64)
+        gated = {
+            (d, b): keep.tile([P, PACK, P], F32, name="gated%d%d" % (d, b), align_bytes=64)
+            for d in range(2)
+            for b in range(BLOCKS)
+        }
+        y = [keep.tile([P, PACK, P], F32, name="y%d" % b, align_bytes=64) for b in range(BLOCKS)]
+        y_rounded = [keep.tile([P, 2 * P, PACK], BF16, name="y_rounded%d" % u, align_bytes=64) for u in range(2)]
+        y_words = keep.tile([P, S], U32, name="y_words", align_bytes=64)
+        y_scales = keep.tile([P, S], U8, name="y_scales", align_bytes=64)
+
+        def bank(n, shape):
+            return psum.tile(shape, F32, name="bank%d" % n, tag="bank%d" % n)
+
+        def load_words(a):
+            nc.sync.dma_start(
+                out=word_table[a][:].bitcast(I32), in_=x_words[a].rearrange("p c r -> p (c r)").bitcast(I32)
+            )
+
+        def load_weights(q):
+            d, h, a = q
+            rows = weights[d][a * P * PACK : (a + 1) * P * PACK, h * HALF : (h + 1) * HALF]
+            nc.sync.dma_start(out=raw[q][:], in_=rows.rearrange("(p j) c -> p j c", j=PACK))
+
+        def interleave(copy, dst, src, c0, c1):
+            copy(
+                dst[:, c0:c1, :].rearrange("p (c i) j -> p c j i", i=4),
+                src[:, :, c0:c1].rearrange("p j (c i) -> p c j i", i=4),
+            )
+
+        def round_weights(q):
+            split = HALF - VECTOR_COLUMNS[pieces.index(q)]
+            if split > 0:
+                interleave(nc.scalar.copy, rounded[q], raw[q], 0, split)
+            if split < HALF:
+                interleave(nc.vector.tensor_copy, rounded[q], raw[q], split, HALF)
+
+        def quantize_weights(q):
+            nc.vector.quantize_mx(
+                out=w_words[q][:].bitcast(FP8X4),
+                scales=w_scales[q][:],
+                in_=rounded[q][:].rearrange("p c j -> p (c j)"),
+            )
+
+        products = {}
+        product_banks = {}
+
+        def multiply(d, h):
+            for a in range(PASSES):
+                for b in range(BLOCKS):
+                    if (d, b) not in product_banks:
+                        product_banks[d, b] = bank(4 * d + b, [P, 2, HALF])
+                    products[d, h, b] = product_banks[d, b][:, h, :]
+                    tokens = slice(b * P, (b + 1) * P)
+                    nc.tensor.matmul_mx(
+                        out=products[d, h, b],
+                        lhsT=picked_words[a][:, tokens].bitcast(FP8X4),
+                        lhsT_scale=picked_scales[4 * a : P, tokens],
+                        rhs=w_words[d, h, a][:].bitcast(FP8X4),
+                        rhs_scale=w_scales[d, h, a][:],
+                        start=(a == 0),
+                        stop=(a == PASSES - 1),
+                    )
+
+        def apply_gate(d, h, b):
+            dealt = products[d, h, b].rearrange("p (l r) -> p r l", r=PACK)
+            dst = gated[d, b][:, :, h * (P // 2) : (h + 1) * (P // 2)]
+            factor = token_gate[:, b, d : d + 1]
+            if (d, h, b) in SCALAR_GATED:
+                positive = keep.tile([P, PACK, P // 2], F32, name="positive%d%d%d" % (d, h, b), align_bytes=64)
+                nc.scalar.activation(out=positive[:], in_=dealt, func=RELU)
+                nc.scalar.activation(out=dst, in_=positive[:], func=COPY, scale=factor)
+            else:
+                nc.vector.tensor_scalar(out=dst, in0=dealt, scalar1=0.0, scalar2=factor, op0=MAX, op1=MULT)
+
+        sums = {}
+
+        def turn(d, b):
+            if d == 0:
+                sums[b] = bank(b, [P, PACK, P])
+            for r in range(PACK):
+                nc.tensor.matmul(
+                    out=sums[b][:, r, :],
+                    lhsT=gated[d, b][:, r, :],
+                    rhs=identity[:],
+                    is_transpose=True,
+                    start=(d == 0 and r == 0),
+                    stop=(d == 1 and r == PACK - 1),
+                )
+
+        nc.vector.memset(scale_table[:].bitcast(I32), 0)
+        nc.vector.memset(gate_table[64:P, :], 0.0)
+        make_identity(nc, identity[:])
+        nc.gpsimd.memset(gate_table[32:64, :], 0.0)
+        nc.sync.dma_start(offsets[:], offs)
+        nc.sync.dma_start(out=gate_table[0:32, :], in_=gate[:, 0:16, :].rearrange("d r c -> r d c"))
+        load_words(0)
+        for quad in range(4):
+            nc.sync.dma_start(
+                out=scale_table[32 * quad : 32 * quad + 4 * PASSES, :].bitcast(I32),
+                in_=x_scales[:, 4 * quad : 4 * quad + 4, :].bitcast(I32),
+            )
+        load_weights((0, 0, 0))
+        load_words(1)
+        load_weights((0, 0, 1))
+        load_weights((0, 1, 0))
+        load_weights((0, 1, 1))
+        load_weights((1, 0, 0))
+        load_weights((1, 0, 1))
+        load_weights((1, 1, 0))
+        load_weights((1, 1, 1))
+
+        nc.vector.tensor_copy(picked_gate[:], gate_table[:].indirect(offsets[:]))
+        nc.vector.tensor_copy(picked_words[0][:], word_table[0][:].indirect(offsets[:]))
+        nc.vector.tensor_copy(picked_scales[:], scale_table[:].indirect(offsets[:]))
+        nc.vector.tensor_copy(picked_words[1][:], word_table[1][:].indirect(offsets[:]))
+        turned_gate = bank(7, [P, BLOCKS, P])
+        for b in range(BLOCKS):
+            nc.tensor.transpose(turned_gate[:, b, :], picked_gate[:, b * P : (b + 1) * P], identity[:])
+        nc.scalar.copy(token_gate[:], turned_gate[:, :, 0:2])
+
+        halves = [(d, h) for d in range(2) for h in range(2)]
+        for a in range(PASSES):
+            round_weights((0, 0, a))
+        for a in range(PASSES):
+            quantize_weights((0, 0, a))
+        for n, (d, h) in enumerate(halves):
+            multiply(d, h)
+            ahead = [halves[n + 1] + (a,) for a in range(PASSES)] if n + 1 < len(halves) else []
+            for q in ahead:
+                round_weights(q)
+            if ahead and QUANTIZE_FIRST[n]:
+                for q in ahead:
+                    quantize_weights(q)
+            for b in range(BLOCKS):
+                apply_gate(d, h, b)
+                if h == 1:
+                    turn(d, b)
+            if ahead and not QUANTIZE_FIRST[n]:
+                for q in ahead:
+                    quantize_weights(q)
+
+        copies = {"S": nc.scalar.copy, "V": nc.vector.tensor_copy}
+        rows_out = out_0.rearrange("(p r) c -> p r c", r=PACK)
+        for b in range(BLOCKS):
+            copies[Y_COPY[b]](y[b][:], sums[b][:])
+            nc.sync.dma_start(out=rows_out[:, :, b * P : (b + 1) * P], in_=y[b][:])
+        for b in range(BLOCKS):
+            pair = y_rounded[b // 2]
+            interleave(copies[Y_ROUND[b]], pair[:, (b % 2) * P : (b % 2 + 1) * P, :], y[b], 0, P)
+            if b % 2 == 1:
+                tokens = slice((b - 1) * P, (b + 1) * P)
+                nc.vector.quantize_mx(
+                    out=y_words[:, tokens].bitcast(FP8X4),
+                    scales=y_scales[:, tokens],
+                    in_=pair[:].rearrange("p c r -> p (c r)"),
+                )
+        words_out = out_1[0].rearrange("p c r -> p (c r)").bitcast(I32)
+        for half in range(2):
+            tokens = slice(half * S // 2, (half + 1) * S // 2)
+            nc.sync.dma_start(out=words_out[:, tokens], in_=y_words[:, tokens].bitcast(I32))
+        for quad in range(4):
+            queue = nc.scalar if quad % 2 else nc.sync
+            queue.dma_start(
+                out=out_2[0, 4 * quad : 4 * quad + 4, :].bitcast(I32),
+                in_=y_scales[32 * quad : 32 * quad + 4, :].bitcast(I32),
+            )

@@ -23,11 +23,11 @@ FP8X4 = mybir.dt.float8_e4m3fn_x4
 MAX = mybir.AluOpType.max
 MULT = mybir.AluOpType.mult
 
-VECTOR_COLUMNS = (128, 0, 128, 0, 160, 96, 0, 256)
-SCALAR_GATED = ((1, 0, 0),)
+VECTOR_COLUMNS = (96, 192, 0, 32, 0, 96, 0, 64)
+SCALAR_GATED = ((1, 0, 0), (1, 0, 1),)
 Y_COPY = "VSSS"
-Y_ROUND = "VVVV"
-QUANTIZE_FIRST = (False, False, True)
+Y_ROUND = "VSVV"
+WHOLE = ((0, 0), (0, 1), (1, 0),)
 RELU = mybir.ActivationFunctionType.Relu
 COPY = mybir.ActivationFunctionType.Copy
 
@@ -47,7 +47,7 @@ def tile_picked_zsmoe_relu_po_kernel(
         word_table = [keep.tile([P, T], U32, name="word_table%d" % a, align_bytes=64) for a in range(PASSES)]
         scale_table = keep.tile([P, T], U8, name="scale_table", align_bytes=64)
         gate_table = keep.tile([P, T], F32, name="gate_table", align_bytes=64)
-        raw = {q: keep.tile([P, PACK, HALF], F32, name="raw%d%d%d" % q, align_bytes=64) for q in pieces}
+        raw = {}
         rounded = {q: keep.tile([P, HALF, PACK], BF16, name="rounded%d%d%d" % q, align_bytes=64) for q in pieces}
         w_words = {q: keep.tile([P, HALF], U32, name="w_words%d%d%d" % q, align_bytes=64) for q in pieces}
         w_scales = {q: keep.tile([P, HALF], U8, name="w_scales%d%d%d" % q, align_bytes=64) for q in pieces}
@@ -61,7 +61,8 @@ def tile_picked_zsmoe_relu_po_kernel(
             for d in range(2)
             for b in range(BLOCKS)
         }
-        y = [keep.tile([P, PACK, P], F32, name="y%d" % b, align_bytes=64) for b in range(BLOCKS)]
+        y_pair = [keep.tile([P, PACK, 2 * P], F32, name="y_pair%d" % u, align_bytes=64) for u in range(2)]
+        y = [y_pair[b // 2][:, :, (b % 2) * P : (b % 2 + 1) * P] for b in range(BLOCKS)]
         y_rounded = [keep.tile([P, 2 * P, PACK], BF16, name="y_rounded%d" % u, align_bytes=64) for u in range(2)]
         y_words = keep.tile([P, S], U32, name="y_words", align_bytes=64)
         y_scales = keep.tile([P, S], U8, name="y_scales", align_bytes=64)
@@ -77,7 +78,16 @@ def tile_picked_zsmoe_relu_po_kernel(
         def load_weights(q):
             d, h, a = q
             rows = weights[d][a * P * PACK : (a + 1) * P * PACK, h * HALF : (h + 1) * HALF]
-            nc.sync.dma_start(out=raw[q][:], in_=rows.rearrange("(p j) c -> p j c", j=PACK))
+            piece = keep.tile([P, PACK, HALF], F32, name="raw%d%d%d" % q, align_bytes=64)
+            nc.sync.dma_start(out=piece[:], in_=rows.rearrange("(p j) c -> p j c", j=PACK))
+            raw[q] = piece[:]
+
+        def load_whole(d, a):
+            rows = weights[d][a * P * PACK : (a + 1) * P * PACK, :]
+            piece = keep.tile([P, PACK, N], F32, name="whole%d%d" % (d, a), align_bytes=64)
+            nc.sync.dma_start(out=piece[:], in_=rows.rearrange("(p j) c -> p j c", j=PACK))
+            for h in range(2):
+                raw[d, h, a] = piece[:, :, h * HALF : (h + 1) * HALF]
 
         def interleave(copy, dst, src, c0, c1):
             copy(
@@ -146,62 +156,69 @@ def tile_picked_zsmoe_relu_po_kernel(
                 )
 
         nc.vector.memset(scale_table[:].bitcast(I32), 0)
-        nc.vector.memset(gate_table[64:P, :], 0.0)
+        nc.vector.memset(gate_table[:].bitcast(I32), 0)
         make_identity(nc, identity[:])
-        nc.gpsimd.memset(gate_table[32:64, :], 0.0)
+        load_whole(0, 0)
+        nc.sync.dma_start(out=gate_table[0:2, :], in_=gate[:, 0, :])
         nc.sync.dma_start(offsets[:], offs)
-        nc.sync.dma_start(out=gate_table[0:32, :], in_=gate[:, 0:16, :].rearrange("d r c -> r d c"))
         load_words(0)
         for quad in range(4):
             nc.sync.dma_start(
                 out=scale_table[32 * quad : 32 * quad + 4 * PASSES, :].bitcast(I32),
                 in_=x_scales[:, 4 * quad : 4 * quad + 4, :].bitcast(I32),
             )
-        load_weights((0, 0, 0))
+        load_whole(0, 1)
         load_words(1)
-        load_weights((0, 0, 1))
-        load_weights((0, 1, 0))
-        load_weights((0, 1, 1))
-        load_weights((1, 0, 0))
+        load_whole(1, 0)
         load_weights((1, 0, 1))
-        load_weights((1, 1, 0))
         load_weights((1, 1, 1))
 
+        nc.vector.tensor_copy(picked_words[1][:], word_table[1][:].indirect(offsets[:]))
         nc.vector.tensor_copy(picked_gate[:], gate_table[:].indirect(offsets[:]))
         nc.vector.tensor_copy(picked_words[0][:], word_table[0][:].indirect(offsets[:]))
         nc.vector.tensor_copy(picked_scales[:], scale_table[:].indirect(offsets[:]))
-        nc.vector.tensor_copy(picked_words[1][:], word_table[1][:].indirect(offsets[:]))
         turned_gate = bank(7, [P, BLOCKS, P])
         for b in range(BLOCKS):
             nc.tensor.transpose(turned_gate[:, b, :], picked_gate[:, b * P : (b + 1) * P], identity[:])
         nc.scalar.copy(token_gate[:], turned_gate[:, :, 0:2])
 
-        halves = [(d, h) for d in range(2) for h in range(2)]
-        for a in range(PASSES):
-            round_weights((0, 0, a))
-        for a in range(PASSES):
-            quantize_weights((0, 0, a))
-        for n, (d, h) in enumerate(halves):
-            multiply(d, h)
-            ahead = [halves[n + 1] + (a,) for a in range(PASSES)] if n + 1 < len(halves) else []
-            for q in ahead:
-                round_weights(q)
-            if ahead and QUANTIZE_FIRST[n]:
-                for q in ahead:
-                    quantize_weights(q)
-            for b in range(BLOCKS):
-                apply_gate(d, h, b)
-                if h == 1:
-                    turn(d, b)
-            if ahead and not QUANTIZE_FIRST[n]:
-                for q in ahead:
-                    quantize_weights(q)
+        round_weights((0, 1, 0))
+        round_weights((0, 0, 0))
+        quantize_weights((0, 1, 0))
+        round_weights((0, 0, 1))
+        quantize_weights((0, 0, 0))
+        quantize_weights((0, 0, 1))
+        round_weights((1, 0, 1))
+        quantize_weights((1, 0, 1))
+        multiply(0, 0)
+        round_weights((0, 1, 1))
+        for b in range(BLOCKS):
+            apply_gate(0, 0, b)
+        round_weights((1, 0, 0))
+        round_weights((1, 1, 0))
+        quantize_weights((0, 1, 1))
+        multiply(0, 1)
+        for b in range(BLOCKS):
+            apply_gate(0, 1, b)
+            turn(0, b)
+        round_weights((1, 1, 1))
+        quantize_weights((1, 0, 0))
+        multiply(1, 0)
+        for b in range(BLOCKS):
+            apply_gate(1, 0, b)
+        quantize_weights((1, 1, 1))
+        quantize_weights((1, 1, 0))
+        multiply(1, 1)
+        for b in range(BLOCKS):
+            apply_gate(1, 1, b)
+            turn(1, b)
 
         copies = {"S": nc.scalar.copy, "V": nc.vector.tensor_copy}
         rows_out = out_0.rearrange("(p r) c -> p r c", r=PACK)
         for b in range(BLOCKS):
-            copies[Y_COPY[b]](y[b][:], sums[b][:])
-            nc.sync.dma_start(out=rows_out[:, :, b * P : (b + 1) * P], in_=y[b][:])
+            copies[Y_COPY[b]](y[b], sums[b][:])
+            if b % 2 == 1:
+                nc.sync.dma_start(out=rows_out[:, :, (b - 1) * P : (b + 1) * P], in_=y_pair[b // 2][:])
         for b in range(BLOCKS):
             pair = y_rounded[b // 2]
             interleave(copies[Y_ROUND[b]], pair[:, (b % 2) * P : (b % 2 + 1) * P, :], y[b], 0, P)
@@ -213,9 +230,7 @@ def tile_picked_zsmoe_relu_po_kernel(
                     in_=pair[:].rearrange("p c r -> p (c r)"),
                 )
         words_out = out_1[0].rearrange("p c r -> p (c r)").bitcast(I32)
-        for half in range(2):
-            tokens = slice(half * S // 2, (half + 1) * S // 2)
-            nc.sync.dma_start(out=words_out[:, tokens], in_=y_words[:, tokens].bitcast(I32))
+        nc.sync.dma_start(out=words_out, in_=y_words[:].bitcast(I32))
         for quad in range(4):
             queue = nc.scalar if quad % 2 else nc.sync
             queue.dma_start(

@@ -23,11 +23,10 @@ FP8X4 = mybir.dt.float8_e4m3fn_x4
 MAX = mybir.AluOpType.max
 MULT = mybir.AluOpType.mult
 
-VECTOR_COLUMNS = (96, 192, 0, 32, 0, 96, 0, 64)
-SCALAR_GATED = ((1, 0, 0), (1, 0, 1),)
-Y_COPY = "VSSS"
-Y_ROUND = "VSVV"
-WHOLE = ((0, 0), (0, 1), (1, 0),)
+VECTOR_COLUMNS = (0, 32, 128, 160, 64, 64, 128, 128)
+SCALAR_GATED = ((0, 0, 0), (1, 0, 0),)
+Y_COPY = "SSSS"
+Y_ROUND = "VVVV"
 RELU = mybir.ActivationFunctionType.Relu
 COPY = mybir.ActivationFunctionType.Copy
 
@@ -61,8 +60,7 @@ def tile_picked_zsmoe_relu_po_kernel(
             for d in range(2)
             for b in range(BLOCKS)
         }
-        y_pair = [keep.tile([P, PACK, 2 * P], F32, name="y_pair%d" % u, align_bytes=64) for u in range(2)]
-        y = [y_pair[b // 2][:, :, (b % 2) * P : (b % 2 + 1) * P] for b in range(BLOCKS)]
+        y = [keep.tile([P, PACK, P], F32, name="y%d" % b, align_bytes=64) for b in range(BLOCKS)]
         y_rounded = [keep.tile([P, 2 * P, PACK], BF16, name="y_rounded%d" % u, align_bytes=64) for u in range(2)]
         y_words = keep.tile([P, S], U32, name="y_words", align_bytes=64)
         y_scales = keep.tile([P, S], U8, name="y_scales", align_bytes=64)
@@ -91,8 +89,8 @@ def tile_picked_zsmoe_relu_po_kernel(
 
         def interleave(copy, dst, src, c0, c1):
             copy(
-                dst[:, c0:c1, :].rearrange("p (c i) j -> p c j i", i=4),
-                src[:, :, c0:c1].rearrange("p j (c i) -> p c j i", i=4),
+                dst[:, c0:c1, :],
+                src[:, :, c0:c1].rearrange("p j c -> p c j"),
             )
 
         def round_weights(q):
@@ -155,59 +153,62 @@ def tile_picked_zsmoe_relu_po_kernel(
                     stop=(d == 1 and r == PACK - 1),
                 )
 
-        nc.vector.memset(scale_table[:].bitcast(I32), 0)
         nc.vector.memset(gate_table[:].bitcast(I32), 0)
+        nc.vector.memset(scale_table[:].bitcast(I32), 0)
         make_identity(nc, identity[:])
-        load_whole(0, 0)
-        nc.sync.dma_start(out=gate_table[0:2, :], in_=gate[:, 0, :])
-        nc.sync.dma_start(offsets[:], offs)
         load_words(0)
+        nc.sync.dma_start(offsets[:], offs)
+        nc.sync.dma_start(out=gate_table[0:2, :], in_=gate[:, 0, :])
+        load_weights((0, 0, 0))
         for quad in range(4):
             nc.sync.dma_start(
                 out=scale_table[32 * quad : 32 * quad + 4 * PASSES, :].bitcast(I32),
                 in_=x_scales[:, 4 * quad : 4 * quad + 4, :].bitcast(I32),
             )
-        load_whole(0, 1)
         load_words(1)
-        load_whole(1, 0)
+        load_weights((0, 0, 1))
+        load_weights((0, 1, 0))
+        load_weights((0, 1, 1))
+        load_weights((1, 0, 0))
         load_weights((1, 0, 1))
+        load_weights((1, 1, 0))
         load_weights((1, 1, 1))
 
-        nc.vector.tensor_copy(picked_words[1][:], word_table[1][:].indirect(offsets[:]))
-        nc.vector.tensor_copy(picked_gate[:], gate_table[:].indirect(offsets[:]))
         nc.vector.tensor_copy(picked_words[0][:], word_table[0][:].indirect(offsets[:]))
+        nc.vector.tensor_copy(picked_gate[:], gate_table[:].indirect(offsets[:]))
         nc.vector.tensor_copy(picked_scales[:], scale_table[:].indirect(offsets[:]))
+        nc.vector.tensor_copy(picked_words[1][:], word_table[1][:].indirect(offsets[:]))
         turned_gate = bank(7, [P, BLOCKS, P])
         for b in range(BLOCKS):
             nc.tensor.transpose(turned_gate[:, b, :], picked_gate[:, b * P : (b + 1) * P], identity[:])
         nc.scalar.copy(token_gate[:], turned_gate[:, :, 0:2])
 
-        round_weights((0, 1, 0))
         round_weights((0, 0, 0))
-        quantize_weights((0, 1, 0))
         round_weights((0, 0, 1))
         quantize_weights((0, 0, 0))
         quantize_weights((0, 0, 1))
-        round_weights((1, 0, 1))
-        quantize_weights((1, 0, 1))
-        multiply(0, 0)
+        round_weights((0, 1, 0))
         round_weights((0, 1, 1))
+        multiply(0, 0)
+        quantize_weights((0, 1, 0))
+        quantize_weights((0, 1, 1))
         for b in range(BLOCKS):
             apply_gate(0, 0, b)
-        round_weights((1, 0, 0))
-        round_weights((1, 1, 0))
-        quantize_weights((0, 1, 1))
         multiply(0, 1)
         for b in range(BLOCKS):
             apply_gate(0, 1, b)
             turn(0, b)
-        round_weights((1, 1, 1))
+        round_weights((1, 0, 0))
+        round_weights((1, 0, 1))
         quantize_weights((1, 0, 0))
+        round_weights((1, 1, 0))
+        quantize_weights((1, 0, 1))
+        round_weights((1, 1, 1))
         multiply(1, 0)
+        quantize_weights((1, 1, 0))
+        quantize_weights((1, 1, 1))
         for b in range(BLOCKS):
             apply_gate(1, 0, b)
-        quantize_weights((1, 1, 1))
-        quantize_weights((1, 1, 0))
         multiply(1, 1)
         for b in range(BLOCKS):
             apply_gate(1, 1, b)
@@ -216,9 +217,8 @@ def tile_picked_zsmoe_relu_po_kernel(
         copies = {"S": nc.scalar.copy, "V": nc.vector.tensor_copy}
         rows_out = out_0.rearrange("(p r) c -> p r c", r=PACK)
         for b in range(BLOCKS):
-            copies[Y_COPY[b]](y[b], sums[b][:])
-            if b % 2 == 1:
-                nc.sync.dma_start(out=rows_out[:, :, (b - 1) * P : (b + 1) * P], in_=y_pair[b // 2][:])
+            copies[Y_COPY[b]](y[b][:], sums[b][:])
+            nc.sync.dma_start(out=rows_out[:, :, b * P : (b + 1) * P], in_=y[b][:])
         for b in range(BLOCKS):
             pair = y_rounded[b // 2]
             interleave(copies[Y_ROUND[b]], pair[:, (b % 2) * P : (b % 2 + 1) * P, :], y[b], 0, P)
@@ -230,7 +230,9 @@ def tile_picked_zsmoe_relu_po_kernel(
                     in_=pair[:].rearrange("p c r -> p (c r)"),
                 )
         words_out = out_1[0].rearrange("p c r -> p (c r)").bitcast(I32)
-        nc.sync.dma_start(out=words_out, in_=y_words[:].bitcast(I32))
+        for half in range(2):
+            tokens = slice(half * S // 2, (half + 1) * S // 2)
+            nc.sync.dma_start(out=words_out[:, tokens], in_=y_words[:, tokens].bitcast(I32))
         for quad in range(4):
             queue = nc.scalar if quad % 2 else nc.sync
             queue.dma_start(

@@ -7,8 +7,13 @@ K, T, S, N = 1024, 1024, 512, 512
 P = 128
 PACK = 4
 PASSES = K // (P * PACK)
-HALF = N // 2
+LAYERS = 2
+HALVES = 2
+HALF = N // HALVES
+WORDS = HALF // PACK
 BLOCKS = S // P
+SIDES = P // WORDS
+BANKS = BLOCKS // SIDES
 
 FLOPS = 2 * 2 * K * N * S
 BYTES = 2 * K * N * 4 + K * T + K * T // 32 + 2 * T * 4 + P * (S // 16) * 2 + N * S * 4 + N * S + N * S // 32
@@ -23,10 +28,8 @@ FP8X4 = mybir.dt.float8_e4m3fn_x4
 MAX = mybir.AluOpType.max
 MULT = mybir.AluOpType.mult
 
-VECTOR_COLUMNS = (0, 32, 128, 160, 64, 64, 128, 128)
-SCALAR_GATED = ((0, 0, 0), (1, 0, 0),)
-Y_COPY = "SSSS"
-Y_ROUND = "VVVV"
+VECTOR_COLUMNS = (0, 96, 0, 0, 0, 0, 0, 0)
+SCALAR_GATED = ()
 RELU = mybir.ActivationFunctionType.Relu
 COPY = mybir.ActivationFunctionType.Copy
 
@@ -36,69 +39,66 @@ def tile_picked_zsmoe_relu_po_kernel(
 ):
     nc = tc.nc
     weights = (w1, w2)
-    pieces = [(d, h, a) for d in range(2) for h in range(2) for a in range(PASSES)]
+    pieces = [(h, d, a) for h in range(HALVES) for d in range(LAYERS) for a in range(PASSES)]
 
     with ExitStack() as ctx:
         keep = ctx.enter_context(tc.tile_pool(name="keep", bufs=1))
+        late = ctx.enter_context(tc.tile_pool(name="late", bufs=1))
         psum = ctx.enter_context(tc.psum_pool(name="psum", bufs=1))
 
-        offsets = keep.tile([P, S // 16], U16, name="offsets")
-        word_table = [keep.tile([P, T], U32, name="word_table%d" % a, align_bytes=64) for a in range(PASSES)]
-        scale_table = keep.tile([P, T], U8, name="scale_table", align_bytes=64)
-        gate_table = keep.tile([P, T], F32, name="gate_table", align_bytes=64)
-        raw = {}
-        rounded = {q: keep.tile([P, HALF, PACK], BF16, name="rounded%d%d%d" % q, align_bytes=64) for q in pieces}
-        w_words = {q: keep.tile([P, HALF], U32, name="w_words%d%d%d" % q, align_bytes=64) for q in pieces}
-        w_scales = {q: keep.tile([P, HALF], U8, name="w_scales%d%d%d" % q, align_bytes=64) for q in pieces}
-        picked_words = [keep.tile([P, S], U32, name="picked_words%d" % a, align_bytes=64) for a in range(PASSES)]
-        picked_scales = keep.tile([P, S], U8, name="picked_scales", align_bytes=64)
-        picked_gate = keep.tile([P, S], F32, name="picked_gate", align_bytes=64)
-        token_gate = keep.tile([P, BLOCKS, 2], F32, name="token_gate", align_bytes=64)
-        identity = keep.tile([P, P], F32, name="identity", align_bytes=64)
-        gated = {
-            (d, b): keep.tile([P, PACK, P], F32, name="gated%d%d" % (d, b), align_bytes=64)
-            for d in range(2)
-            for b in range(BLOCKS)
-        }
-        y = [keep.tile([P, PACK, P], F32, name="y%d" % b, align_bytes=64) for b in range(BLOCKS)]
-        y_rounded = [keep.tile([P, 2 * P, PACK], BF16, name="y_rounded%d" % u, align_bytes=64) for u in range(2)]
-        y_words = keep.tile([P, S], U32, name="y_words", align_bytes=64)
-        y_scales = keep.tile([P, S], U8, name="y_scales", align_bytes=64)
+        def tile(shape, dtype, name):
+            return keep.tile(shape, dtype, name=name, align_bytes=64)
 
-        def bank(n, shape):
-            return psum.tile(shape, F32, name="bank%d" % n, tag="bank%d" % n)
+        offsets = keep.tile([P, S // 16], U16, name="offsets")
+        word_table = [tile([P, T], U32, "word_table%d" % a) for a in range(PASSES)]
+        scale_table = tile([P, T], U8, "scale_table")
+        gate_table = tile([P, T], F32, "gate_table")
+        raw = {}
+        rounded = {q: tile([P, HALF, PACK], BF16, "rounded%d%d%d" % q) for q in pieces}
+        w_words = {q: tile([P, HALF], U32, "w_words%d%d%d" % q) for q in pieces}
+        w_scales = {q: tile([P, HALF], U8, "w_scales%d%d%d" % q) for q in pieces}
+        picked_words = [tile([P, S], U32, "picked_words%d" % a) for a in range(PASSES)]
+        picked_scales = tile([P, S], U8, "picked_scales")
+        picked_gate = tile([P, S], F32, "picked_gate")
+        identity = tile([P, P], F32, "identity")
+        gated = {}
+        y = {}
+        y_rounded = {}
+        y_words = [tile([P, BANKS * P], U32, "y_words%d" % h) for h in range(HALVES)]
+        y_scales = tile([P, HALVES, BANKS * P], U8, "y_scales")
+
+        def bank(name, shape):
+            return psum.tile(shape, F32, name=name, tag=name)
 
         def load_words(a):
             nc.sync.dma_start(
                 out=word_table[a][:].bitcast(I32), in_=x_words[a].rearrange("p c r -> p (c r)").bitcast(I32)
             )
 
-        def load_weights(q):
-            d, h, a = q
+        def load_half(h, d, a):
             rows = weights[d][a * P * PACK : (a + 1) * P * PACK, h * HALF : (h + 1) * HALF]
-            piece = keep.tile([P, PACK, HALF], F32, name="raw%d%d%d" % q, align_bytes=64)
+            if (h, d, a) == pieces[-1]:
+                piece = late.tile([P, PACK, HALF], F32, name="raw_last", offset=0, align_bytes=64)
+            else:
+                piece = tile([P, PACK, HALF], F32, "raw%d%d%d" % (h, d, a))
             nc.sync.dma_start(out=piece[:], in_=rows.rearrange("(p j) c -> p j c", j=PACK))
-            raw[q] = piece[:]
+            raw[h, d, a] = piece[:]
 
-        def load_whole(d, a):
+        def load_pass(d, a):
             rows = weights[d][a * P * PACK : (a + 1) * P * PACK, :]
-            piece = keep.tile([P, PACK, N], F32, name="whole%d%d" % (d, a), align_bytes=64)
+            piece = tile([P, PACK, N], F32, "whole%d%d" % (d, a))
             nc.sync.dma_start(out=piece[:], in_=rows.rearrange("(p j) c -> p j c", j=PACK))
-            for h in range(2):
-                raw[d, h, a] = piece[:, :, h * HALF : (h + 1) * HALF]
+            for h in range(HALVES):
+                raw[h, d, a] = piece[:, :, h * HALF : (h + 1) * HALF]
 
-        def interleave(copy, dst, src, c0, c1):
-            copy(
-                dst[:, c0:c1, :],
-                src[:, :, c0:c1].rearrange("p j c -> p c j"),
-            )
+        def interleave(copy, dst, src):
+            copy(dst.rearrange("p (c i) j -> p c j i", i=2), src.rearrange("p j (c i) -> p c j i", i=2))
 
         def round_weights(q):
             split = HALF - VECTOR_COLUMNS[pieces.index(q)]
-            if split > 0:
-                interleave(nc.scalar.copy, rounded[q], raw[q], 0, split)
-            if split < HALF:
-                interleave(nc.vector.tensor_copy, rounded[q], raw[q], split, HALF)
+            for copy, c0, c1 in ((nc.scalar.copy, 0, split), (nc.vector.tensor_copy, split, HALF)):
+                if c0 < c1:
+                    interleave(copy, rounded[q][:, c0:c1, :], raw[q][:, :, c0:c1])
 
         def quantize_weights(q):
             nc.vector.quantize_mx(
@@ -108,134 +108,165 @@ def tile_picked_zsmoe_relu_po_kernel(
             )
 
         products = {}
-        product_banks = {}
 
-        def multiply(d, h):
-            for a in range(PASSES):
-                for b in range(BLOCKS):
-                    if (d, b) not in product_banks:
-                        product_banks[d, b] = bank(4 * d + b, [P, 2, HALF])
-                    products[d, h, b] = product_banks[d, b][:, h, :]
+        def multiply(q, banks):
+            h, d, a = q
+            for u in banks:
+                for side in range(SIDES):
+                    b = SIDES * side + u
+                    if a == 0:
+                        products[h, d, b] = bank("product%d" % b, [P, HALF])
                     tokens = slice(b * P, (b + 1) * P)
                     nc.tensor.matmul_mx(
-                        out=products[d, h, b],
+                        out=products[h, d, b][:],
                         lhsT=picked_words[a][:, tokens].bitcast(FP8X4),
                         lhsT_scale=picked_scales[4 * a : P, tokens],
-                        rhs=w_words[d, h, a][:].bitcast(FP8X4),
-                        rhs_scale=w_scales[d, h, a][:],
+                        rhs=w_words[q][:].bitcast(FP8X4),
+                        rhs_scale=w_scales[q][:],
                         start=(a == 0),
                         stop=(a == PASSES - 1),
                     )
 
-        def apply_gate(d, h, b):
-            dealt = products[d, h, b].rearrange("p (l r) -> p r l", r=PACK)
-            dst = gated[d, b][:, :, h * (P // 2) : (h + 1) * (P // 2)]
-            factor = token_gate[:, b, d : d + 1]
-            if (d, h, b) in SCALAR_GATED:
-                positive = keep.tile([P, PACK, P // 2], F32, name="positive%d%d%d" % (d, h, b), align_bytes=64)
-                nc.scalar.activation(out=positive[:], in_=dealt, func=RELU)
-                nc.scalar.activation(out=dst, in_=positive[:], func=COPY, scale=factor)
-            else:
-                nc.vector.tensor_scalar(out=dst, in0=dealt, scalar1=0.0, scalar2=factor, op0=MAX, op1=MULT)
-
         sums = {}
 
-        def turn(d, b):
-            if d == 0:
-                sums[b] = bank(b, [P, PACK, P])
-            for r in range(PACK):
-                nc.tensor.matmul(
-                    out=sums[b][:, r, :],
-                    lhsT=gated[d, b][:, r, :],
-                    rhs=identity[:],
-                    is_transpose=True,
-                    start=(d == 0 and r == 0),
-                    stop=(d == 1 and r == PACK - 1),
-                )
+        def apply_gate(h, d, u, tag):
+            if tag == "raw111":
+                gated[h, d, u] = late.tile([P, PACK, SIDES, WORDS], F32, name="gated101", offset=0, align_bytes=64)
+            else:
+                gated[h, d, u] = keep.tile([P, PACK, SIDES, WORDS], F32, name="gated%d%d%d" % (h, d, u), tag=tag, align_bytes=64)
+            if True:
+                for side in range(SIDES):
+                    b = SIDES * side + u
+                    dealt = products[h, d, b][:].rearrange("p (i t) -> p t i", t=PACK)
+                    dst = gated[h, d, u][:, :, side, :]
+                    factor = token_gate[:, b, d : d + 1]
+                    if (h, d, b) in SCALAR_GATED:
+                        positive = tile([P, PACK, WORDS], F32, "positive%d%d%d" % (h, d, b))
+                        nc.scalar.activation(out=positive[:], in_=dealt, func=RELU)
+                        nc.scalar.activation(out=dst, in_=positive[:], func=COPY, scale=factor)
+                    else:
+                        nc.vector.tensor_scalar(out=dst, in0=dealt, scalar1=0.0, scalar2=factor, op0=MAX, op1=MULT)
 
-        nc.vector.memset(gate_table[:].bitcast(I32), 0)
+        def turn(h, d, u):
+            if True:
+                if d == 0:
+                    sums[h, u] = bank("sum%d" % (BANKS * h + u), [P, PACK, P])
+                for t in range(PACK):
+                    nc.tensor.matmul(
+                        out=sums[h, u][:, t, :],
+                        lhsT=gated[h, d, u][:, t, :, :].rearrange("p s i -> p (s i)"),
+                        rhs=identity[:],
+                        is_transpose=True,
+                        start=(d == 0 and t == 0),
+                        stop=(d == LAYERS - 1 and t == PACK - 1),
+                    )
+
+        def copy_sum(copy, h, u):
+            if h not in y:
+                y[h] = late.tile([P, PACK, BANKS, P], F32, name="y%d" % h, offset=2048 + 4096 * h, align_bytes=64)
+            copy(y[h][:, :, u, :], sums[h, u][:])
+
+        def rounded_sum(h, u):
+            if h not in y_rounded:
+                y_rounded[h] = keep.tile([P, BANKS * P, PACK], BF16, name="y_rounded%d" % h, tag="y_rounded%d" % h, align_bytes=64)
+            return y_rounded[h][:, u * P : (u + 1) * P, :]
+
+        def round_from_bank(copy, h, u):
+            copy(rounded_sum(h, u), sums[h, u][:].rearrange("p t j -> p j t"))
+
+        def round_from_copy(copy, h, u):
+            interleave(copy, rounded_sum(h, u), y[h][:, :, u, :])
+
+        def quantize_sum(h, u0, u1):
+            nc.vector.quantize_mx(
+                out=y_words[h][:, u0 * P : u1 * P].bitcast(FP8X4),
+                scales=y_scales[:, h, u0 * P : u1 * P],
+                in_=y_rounded[h][:, u0 * P : u1 * P, :].rearrange("p c t -> p (c t)"),
+            )
+
+        def store_values(h):
+            rows = out_0[h * HALF : (h + 1) * HALF, :].rearrange("(i t) c -> i t c", t=PACK)
+            for side in range(SIDES):
+                held = slice(side * WORDS, (side + 1) * WORDS)
+                tokens = slice(side * BANKS * P, (side + 1) * BANKS * P)
+                queue = nc.scalar if side else nc.sync
+                queue.dma_start(out=rows[:, :, tokens], in_=y[h][held].rearrange("p t u j -> p t (u j)"))
+
+        def store_words(h):
+            words = out_1[0, h * WORDS : (h + 1) * WORDS].rearrange("i c r -> i (c r)").bitcast(I32)
+            for side in range(SIDES):
+                held = slice(side * WORDS, (side + 1) * WORDS)
+                tokens = slice(side * BANKS * P, (side + 1) * BANKS * P)
+                queue = nc.scalar if side and h else nc.sync
+                queue.dma_start(out=words[:, tokens], in_=y_words[h][held].bitcast(I32))
+
         nc.vector.memset(scale_table[:].bitcast(I32), 0)
+        nc.vector.memset(gate_table[:].bitcast(I32), 0)
         make_identity(nc, identity[:])
         load_words(0)
         nc.sync.dma_start(offsets[:], offs)
-        nc.sync.dma_start(out=gate_table[0:2, :], in_=gate[:, 0, :])
-        load_weights((0, 0, 0))
         for quad in range(4):
             nc.sync.dma_start(
                 out=scale_table[32 * quad : 32 * quad + 4 * PASSES, :].bitcast(I32),
                 in_=x_scales[:, 4 * quad : 4 * quad + 4, :].bitcast(I32),
             )
+        nc.sync.dma_start(out=gate_table[0:LAYERS, :], in_=gate[:, 0, :])
+        load_half(*pieces[0])
         load_words(1)
-        load_weights((0, 0, 1))
-        load_weights((0, 1, 0))
-        load_weights((0, 1, 1))
-        load_weights((1, 0, 0))
-        load_weights((1, 0, 1))
-        load_weights((1, 1, 0))
-        load_weights((1, 1, 1))
+        for q in pieces[1:]:
+            load_half(*q)
 
         nc.vector.tensor_copy(picked_words[0][:], word_table[0][:].indirect(offsets[:]))
-        nc.vector.tensor_copy(picked_gate[:], gate_table[:].indirect(offsets[:]))
         nc.vector.tensor_copy(picked_scales[:], scale_table[:].indirect(offsets[:]))
+        nc.vector.tensor_copy(picked_gate[:], gate_table[:].indirect(offsets[:]))
         nc.vector.tensor_copy(picked_words[1][:], word_table[1][:].indirect(offsets[:]))
-        turned_gate = bank(7, [P, BLOCKS, P])
+        turned_gate = bank("sum0", [P, BLOCKS, P])
         for b in range(BLOCKS):
             nc.tensor.transpose(turned_gate[:, b, :], picked_gate[:, b * P : (b + 1) * P], identity[:])
-        nc.scalar.copy(token_gate[:], turned_gate[:, :, 0:2])
+        round_weights(pieces[0])
+        round_weights(pieces[1])
+        token_gate = keep.tile([P, BLOCKS, LAYERS], F32, name="token_gate", tag="raw001", align_bytes=64)
+        nc.scalar.copy(token_gate[:], turned_gate[:, :, 0:LAYERS])
 
-        round_weights((0, 0, 0))
-        round_weights((0, 0, 1))
-        quantize_weights((0, 0, 0))
-        quantize_weights((0, 0, 1))
-        round_weights((0, 1, 0))
-        round_weights((0, 1, 1))
-        multiply(0, 0)
-        quantize_weights((0, 1, 0))
-        quantize_weights((0, 1, 1))
-        for b in range(BLOCKS):
-            apply_gate(0, 0, b)
-        multiply(0, 1)
-        for b in range(BLOCKS):
-            apply_gate(0, 1, b)
-            turn(0, b)
-        round_weights((1, 0, 0))
-        round_weights((1, 0, 1))
-        quantize_weights((1, 0, 0))
-        round_weights((1, 1, 0))
-        quantize_weights((1, 0, 1))
-        round_weights((1, 1, 1))
-        multiply(1, 0)
-        quantize_weights((1, 1, 0))
-        quantize_weights((1, 1, 1))
-        for b in range(BLOCKS):
-            apply_gate(1, 0, b)
-        multiply(1, 1)
-        for b in range(BLOCKS):
-            apply_gate(1, 1, b)
-            turn(1, b)
-
-        copies = {"S": nc.scalar.copy, "V": nc.vector.tensor_copy}
-        rows_out = out_0.rearrange("(p r) c -> p r c", r=PACK)
-        for b in range(BLOCKS):
-            copies[Y_COPY[b]](y[b][:], sums[b][:])
-            nc.sync.dma_start(out=rows_out[:, :, b * P : (b + 1) * P], in_=y[b][:])
-        for b in range(BLOCKS):
-            pair = y_rounded[b // 2]
-            interleave(copies[Y_ROUND[b]], pair[:, (b % 2) * P : (b % 2 + 1) * P, :], y[b], 0, P)
-            if b % 2 == 1:
-                tokens = slice((b - 1) * P, (b + 1) * P)
-                nc.vector.quantize_mx(
-                    out=y_words[:, tokens].bitcast(FP8X4),
-                    scales=y_scales[:, tokens],
-                    in_=pair[:].rearrange("p c r -> p (c r)"),
-                )
-        words_out = out_1[0].rearrange("p c r -> p (c r)").bitcast(I32)
-        for half in range(2):
-            tokens = slice(half * S // 2, (half + 1) * S // 2)
-            nc.sync.dma_start(out=words_out[:, tokens], in_=y_words[:, tokens].bitcast(I32))
+        steps = [(h, d) for h in range(HALVES) for d in range(LAYERS)]
+        quantize_weights(pieces[0])
+        multiply(pieces[0], (0, 1))
+        quantize_weights(pieces[1])
+        multiply(pieces[1], (0, 1))
+        for n, step in enumerate(steps):
+            last = n == len(steps) - 1
+            apply_gate(*step, 0, "gated%d%d0" % step)
+            if not last:
+                nxt = steps[n + 1]
+                for a in range(PASSES):
+                    round_weights(nxt + (a,))
+                    quantize_weights(nxt + (a,))
+                    multiply(nxt + (a,), (0,))
+            apply_gate(*step, 1, "gated%d%d1" % step if last else "raw%d%d1" % nxt)
+            if not last:
+                for a in range(PASSES):
+                    multiply(nxt + (a,), (1,))
+            turn(*step, 0)
+            turn(*step, 1)
+        for u in range(BANKS):
+            copy_sum(nc.scalar.copy, 0, u)
+        for u in range(BANKS):
+            round_from_copy(nc.scalar.copy, 0, u)
+        store_values(0)
+        quantize_sum(0, 0, BANKS)
+        store_words(0)
+        for u in range(BANKS):
+            copy_sum(nc.scalar.copy, 1, u)
+            round_from_copy(nc.vector.tensor_copy, 1, u)
+            quantize_sum(1, u, u + 1)
+        store_values(1)
+        store_words(1)
+        scale_rows = out_2[0].rearrange("(h g r) c -> g r h c", h=HALVES, r=4)
         for quad in range(4):
+            side, group = divmod(quad, 2)
+            tokens = slice(side * BANKS * P, (side + 1) * BANKS * P)
             queue = nc.scalar if quad % 2 else nc.sync
             queue.dma_start(
-                out=out_2[0, 4 * quad : 4 * quad + 4, :].bitcast(I32),
-                in_=y_scales[32 * quad : 32 * quad + 4, :].bitcast(I32),
+                out=scale_rows[group][:, :, tokens].bitcast(I32),
+                in_=y_scales[32 * quad : 32 * quad + 4].bitcast(I32),
             )

@@ -28,7 +28,7 @@ FP8X4 = mybir.dt.float8_e4m3fn_x4
 MAX = mybir.AluOpType.max
 MULT = mybir.AluOpType.mult
 
-VECTOR_COLUMNS = (0, 96, 0, 0, 0, 0, 0, 0)
+VECTOR_COLUMNS = (0, 96, 0, 64, 0, 64, 0, 64)
 SCALAR_GATED = ()
 RELU = mybir.ActivationFunctionType.Relu
 COPY = mybir.ActivationFunctionType.Copy
@@ -95,10 +95,10 @@ def tile_picked_zsmoe_relu_po_kernel(
             copy(dst.rearrange("p (c i) j -> p c j i", i=2), src.rearrange("p j (c i) -> p c j i", i=2))
 
         def round_weights(q):
-            split = HALF - VECTOR_COLUMNS[pieces.index(q)]
-            for copy, c0, c1 in ((nc.scalar.copy, 0, split), (nc.vector.tensor_copy, split, HALF)):
-                if c0 < c1:
-                    interleave(copy, rounded[q][:, c0:c1, :], raw[q][:, :, c0:c1])
+            vector_from = HALF - VECTOR_COLUMNS[pieces.index(q)]
+            interleave(nc.scalar.copy, rounded[q][:, :vector_from, :], raw[q][:, :, :vector_from])
+            if vector_from < HALF:
+                interleave(nc.vector.tensor_copy, rounded[q][:, vector_from:, :], raw[q][:, :, vector_from:])
 
         def quantize_weights(q):
             nc.vector.quantize_mx(
@@ -229,13 +229,15 @@ def tile_picked_zsmoe_relu_po_kernel(
         nc.scalar.copy(token_gate[:], turned_gate[:, :, 0:LAYERS])
 
         steps = [(h, d) for h in range(HALVES) for d in range(LAYERS)]
-        quantize_weights(pieces[0])
-        multiply(pieces[0], (0, 1))
-        quantize_weights(pieces[1])
-        multiply(pieces[1], (0, 1))
+        for q in pieces[:PASSES]:
+            quantize_weights(q)
+            multiply(q, (0, 1))
         for n, step in enumerate(steps):
             last = n == len(steps) - 1
             apply_gate(*step, 0, "gated%d%d0" % step)
+            if n > 0:
+                turn(*steps[n - 1], 1)
+            turn(*step, 0)
             if not last:
                 nxt = steps[n + 1]
                 for a in range(PASSES):
@@ -246,8 +248,7 @@ def tile_picked_zsmoe_relu_po_kernel(
             if not last:
                 for a in range(PASSES):
                     multiply(nxt + (a,), (1,))
-            turn(*step, 0)
-            turn(*step, 1)
+        turn(*steps[-1], 1)
         for u in range(BANKS):
             copy_sum(nc.scalar.copy, 0, u)
         for u in range(BANKS):

@@ -28,7 +28,7 @@ FP8X4 = mybir.dt.float8_e4m3fn_x4
 MAX = mybir.AluOpType.max
 MULT = mybir.AluOpType.mult
 
-VECTOR_COLUMNS = (0, 96, 0, 64, 0, 64, 0, 64)
+VECTOR_COLUMNS = (0, 0, 0, 96, 0, 96, 0, 96)
 SCALAR_GATED = ()
 RELU = mybir.ActivationFunctionType.Relu
 COPY = mybir.ActivationFunctionType.Copy
@@ -57,7 +57,7 @@ def tile_picked_zsmoe_relu_po_kernel(
         rounded = {q: tile([P, HALF, PACK], BF16, "rounded%d%d%d" % q) for q in pieces}
         w_words = {q: tile([P, HALF], U32, "w_words%d%d%d" % q) for q in pieces}
         w_scales = {q: tile([P, HALF], U8, "w_scales%d%d%d" % q) for q in pieces}
-        picked_words = [tile([P, S], U32, "picked_words%d" % a) for a in range(PASSES)]
+        picked_words = [tile([P, S], U32, "picked_words0")]
         picked_scales = tile([P, S], U8, "picked_scales")
         picked_gate = tile([P, S], F32, "picked_gate")
         identity = tile([P, P], F32, "identity")
@@ -200,38 +200,44 @@ def tile_picked_zsmoe_relu_po_kernel(
                 queue = nc.scalar if side and h else nc.sync
                 queue.dma_start(out=words[:, tokens], in_=y_words[h][held].bitcast(I32))
 
+        warm = tile([P, 16], F32, "warm")
+        nc.gpsimd.memset(warm[:, 0:8], 0.0)
+        nc.scalar.copy(warm[:, 8:16], warm[:, 0:8])
         nc.vector.memset(scale_table[:].bitcast(I32), 0)
         nc.vector.memset(gate_table[:].bitcast(I32), 0)
         make_identity(nc, identity[:])
-        load_words(0)
         nc.sync.dma_start(offsets[:], offs)
+        load_words(0)
+        nc.sync.dma_start(out=gate_table[0:LAYERS, :], in_=gate[:, 0, :])
         for quad in range(4):
             nc.sync.dma_start(
                 out=scale_table[32 * quad : 32 * quad + 4 * PASSES, :].bitcast(I32),
                 in_=x_scales[:, 4 * quad : 4 * quad + 4, :].bitcast(I32),
             )
-        nc.sync.dma_start(out=gate_table[0:LAYERS, :], in_=gate[:, 0, :])
         load_half(*pieces[0])
+        load_half(*pieces[1])
         load_words(1)
-        for q in pieces[1:]:
+        for q in pieces[2:]:
             load_half(*q)
 
         nc.vector.tensor_copy(picked_words[0][:], word_table[0][:].indirect(offsets[:]))
-        nc.vector.tensor_copy(picked_scales[:], scale_table[:].indirect(offsets[:]))
         nc.vector.tensor_copy(picked_gate[:], gate_table[:].indirect(offsets[:]))
-        nc.vector.tensor_copy(picked_words[1][:], word_table[1][:].indirect(offsets[:]))
+        nc.vector.tensor_copy(picked_scales[:], scale_table[:].indirect(offsets[:]))
         turned_gate = bank("sum0", [P, BLOCKS, P])
         for b in range(BLOCKS):
             nc.tensor.transpose(turned_gate[:, b, :], picked_gate[:, b * P : (b + 1) * P], identity[:])
         round_weights(pieces[0])
+        quantize_weights(pieces[0])
+        multiply(pieces[0], (0, 1))
+        picked_words.append(keep.tile([P, S], U32, name="picked_words1", tag="picked_words1", align_bytes=64))
+        nc.vector.tensor_copy(picked_words[1][:], word_table[1][:].indirect(offsets[:]))
         round_weights(pieces[1])
         token_gate = keep.tile([P, BLOCKS, LAYERS], F32, name="token_gate", tag="raw001", align_bytes=64)
         nc.scalar.copy(token_gate[:], turned_gate[:, :, 0:LAYERS])
+        quantize_weights(pieces[1])
+        multiply(pieces[1], (0, 1))
 
         steps = [(h, d) for h in range(HALVES) for d in range(LAYERS)]
-        for q in pieces[:PASSES]:
-            quantize_weights(q)
-            multiply(q, (0, 1))
         for n, step in enumerate(steps):
             last = n == len(steps) - 1
             apply_gate(*step, 0, "gated%d%d0" % step)

@@ -28,7 +28,7 @@ FP8X4 = mybir.dt.float8_e4m3fn_x4
 MAX = mybir.AluOpType.max
 MULT = mybir.AluOpType.mult
 
-VECTOR_COLUMNS = (0, 0, 0, 96, 0, 96, 0, 96)
+VECTOR_COLUMNS = (0, 0, 0, 96, 0, 96, 0, 128)
 SCALAR_GATED = ()
 RELU = mybir.ActivationFunctionType.Relu
 COPY = mybir.ActivationFunctionType.Copy
@@ -148,31 +148,32 @@ def tile_picked_zsmoe_relu_po_kernel(
                         nc.vector.tensor_scalar(out=dst, in0=dealt, scalar1=0.0, scalar2=factor, op0=MAX, op1=MULT)
 
         def turn(h, d, u):
-            if True:
-                if d == 0:
-                    sums[h, u] = bank("sum%d" % (BANKS * h + u), [P, PACK, P])
-                for t in range(PACK):
-                    nc.tensor.matmul(
-                        out=sums[h, u][:, t, :],
-                        lhsT=gated[h, d, u][:, t, :, :].rearrange("p s i -> p (s i)"),
-                        rhs=identity[:],
-                        is_transpose=True,
-                        start=(d == 0 and t == 0),
-                        stop=(d == LAYERS - 1 and t == PACK - 1),
-                    )
+            if d == 0:
+                if (h, u) == (HALVES - 1, BANKS - 1):
+                    sums[h, u] = [bank(name, [P, 2, P]) for name in ("sum3", "sum0")]
+                else:
+                    sums[h, u] = [bank("sum%d" % (BANKS * h + u), [P, PACK, P])]
+            share = PACK // len(sums[h, u])
+            for t in range(PACK):
+                nc.tensor.matmul(
+                    out=sums[h, u][t // share][:, t % share, :],
+                    lhsT=gated[h, d, u][:, t, :, :].rearrange("p s i -> p (s i)"),
+                    rhs=identity[:],
+                    is_transpose=True,
+                    start=(d == 0 and t % share == 0),
+                    stop=(d == LAYERS - 1 and t % share == share - 1),
+                )
 
-        def copy_sum(copy, h, u):
+        def copy_sum(copy, h, u, part=0):
             if h not in y:
                 y[h] = late.tile([P, PACK, BANKS, P], F32, name="y%d" % h, offset=2048 + 4096 * h, align_bytes=64)
-            copy(y[h][:, :, u, :], sums[h, u][:])
+            share = PACK // len(sums[h, u])
+            copy(y[h][:, part * share : (part + 1) * share, u, :], sums[h, u][part][:])
 
         def rounded_sum(h, u):
             if h not in y_rounded:
                 y_rounded[h] = keep.tile([P, BANKS * P, PACK], BF16, name="y_rounded%d" % h, tag="y_rounded%d" % h, align_bytes=64)
             return y_rounded[h][:, u * P : (u + 1) * P, :]
-
-        def round_from_bank(copy, h, u):
-            copy(rounded_sum(h, u), sums[h, u][:].rearrange("p t j -> p j t"))
 
         def round_from_copy(copy, h, u):
             interleave(copy, rounded_sum(h, u), y[h][:, :, u, :])
@@ -201,19 +202,20 @@ def tile_picked_zsmoe_relu_po_kernel(
                 queue.dma_start(out=words[:, tokens], in_=y_words[h][held].bitcast(I32))
 
         warm = tile([P, 16], F32, "warm")
-        nc.gpsimd.memset(warm[:, 0:8], 0.0)
+        nc.vector.memset(warm[:, 0:8], 0.0)
         nc.scalar.copy(warm[:, 8:16], warm[:, 0:8])
         nc.vector.memset(scale_table[:].bitcast(I32), 0)
         nc.vector.memset(gate_table[:].bitcast(I32), 0)
-        make_identity(nc, identity[:])
+        nc.vector.memset(identity[:], 0.0)
+        make_identity(nc, identity[:], nomemset=True)
         nc.sync.dma_start(offsets[:], offs)
         load_words(0)
-        nc.sync.dma_start(out=gate_table[0:LAYERS, :], in_=gate[:, 0, :])
         for quad in range(4):
             nc.sync.dma_start(
                 out=scale_table[32 * quad : 32 * quad + 4 * PASSES, :].bitcast(I32),
                 in_=x_scales[:, 4 * quad : 4 * quad + 4, :].bitcast(I32),
             )
+        nc.sync.dma_start(out=gate_table[0:LAYERS, :], in_=gate[:, 0, :])
         load_half(*pieces[0])
         load_half(*pieces[1])
         load_words(1)
@@ -221,8 +223,8 @@ def tile_picked_zsmoe_relu_po_kernel(
             load_half(*q)
 
         nc.vector.tensor_copy(picked_words[0][:], word_table[0][:].indirect(offsets[:]))
-        nc.vector.tensor_copy(picked_gate[:], gate_table[:].indirect(offsets[:]))
         nc.vector.tensor_copy(picked_scales[:], scale_table[:].indirect(offsets[:]))
+        nc.vector.tensor_copy(picked_gate[:], gate_table[:].indirect(offsets[:]))
         turned_gate = bank("sum0", [P, BLOCKS, P])
         for b in range(BLOCKS):
             nc.tensor.transpose(turned_gate[:, b, :], picked_gate[:, b * P : (b + 1) * P], identity[:])
@@ -262,11 +264,13 @@ def tile_picked_zsmoe_relu_po_kernel(
         store_values(0)
         quantize_sum(0, 0, BANKS)
         store_words(0)
-        for u in range(BANKS):
-            copy_sum(nc.scalar.copy, 1, u)
-            round_from_copy(nc.vector.tensor_copy, 1, u)
-            quantize_sum(1, u, u + 1)
+        copy_sum(nc.scalar.copy, 1, 0)
+        copy_sum(nc.vector.tensor_copy, 1, 1, 0)
+        copy_sum(nc.scalar.copy, 1, 1, 1)
         store_values(1)
+        round_from_copy(nc.vector.tensor_copy, 1, 0)
+        round_from_copy(nc.vector.tensor_copy, 1, 1)
+        quantize_sum(1, 0, BANKS)
         store_words(1)
         scale_rows = out_2[0].rearrange("(h g r) c -> g r h c", h=HALVES, r=4)
         for quad in range(4):

@@ -208,8 +208,8 @@ def tile_picked_zsmoe_relu_po_kernel(
         nc.vector.memset(gate_table[:].bitcast(I32), 0)
         nc.vector.memset(identity[:], 0.0)
         make_identity(nc, identity[:], nomemset=True)
-        nc.sync.dma_start(offsets[:], offs)
         load_words(0)
+        nc.sync.dma_start(offsets[:], offs)
         for quad in range(4):
             nc.sync.dma_start(
                 out=scale_table[32 * quad : 32 * quad + 4 * PASSES, :].bitcast(I32),

@@ -231,13 +231,20 @@ def tile_picked_zsmoe_relu_po_kernel(
         round_weights(pieces[0])
         quantize_weights(pieces[0])
         multiply(pieces[0], (0, 1))
-        picked_words.append(keep.tile([P, S], U32, name="picked_words1", tag="picked_words1", align_bytes=64))
-        nc.vector.tensor_copy(picked_words[1][:], word_table[1][:].indirect(offsets[:]))
+        picked_words.append(tile([P, S], U32, "picked_words1"))
         round_weights(pieces[1])
         token_gate = keep.tile([P, BLOCKS, LAYERS], F32, name="token_gate", tag="raw001", align_bytes=64)
         nc.scalar.copy(token_gate[:], turned_gate[:, :, 0:LAYERS])
-        quantize_weights(pieces[1])
-        multiply(pieces[1], (0, 1))
+        for u in range(BANKS):
+            for side in range(SIDES):
+                b = BANKS * side + u
+                nc.vector.tensor_copy(
+                    picked_words[1][:, b * P : (b + 1) * P],
+                    word_table[1][:].indirect(offsets[:, b * P // 16 : (b + 1) * P // 16]),
+                )
+            if u == 0:
+                quantize_weights(pieces[1])
+            multiply(pieces[1], (u,))
 
         steps = [(h, d) for h in range(HALVES) for d in range(LAYERS)]
         for n, step in enumerate(steps):

@@ -6,6 +6,9 @@ from concourse.masks import make_identity
 K, T, S, N = 1024, 1024, 512, 512
 P = 128
 PACK = 4
+LIST_ROWS = 16
+QUADRANT = 32
+SCALE_ROWS = 4
 PASSES = K // (P * PACK)
 LAYERS = 2
 HALVES = 2
@@ -13,7 +16,7 @@ HALF = N // HALVES
 WORDS = HALF // PACK
 BLOCKS = S // P
 SIDES = P // WORDS
-BANKS = BLOCKS // SIDES
+PAIRS = BLOCKS // SIDES
 
 FLOPS = 2 * 2 * K * N * S
 BYTES = 2 * K * N * 4 + K * T + K * T // 32 + 2 * T * 4 + P * (S // 16) * 2 + N * S * 4 + N * S + N * S // 32
@@ -28,10 +31,10 @@ FP8X4 = mybir.dt.float8_e4m3fn_x4
 MAX = mybir.AluOpType.max
 MULT = mybir.AluOpType.mult
 
-VECTOR_COLUMNS = (0, 0, 0, 96, 0, 96, 0, 128)
-SCALAR_GATED = ()
-RELU = mybir.ActivationFunctionType.Relu
-COPY = mybir.ActivationFunctionType.Copy
+VECTOR_COLUMNS = 96
+VECTOR_COLUMNS_LAST = 128
+GATED_BYTES = PACK * P * 4
+Y_BYTES = PAIRS * GATED_BYTES
 
 
 def tile_picked_zsmoe_relu_po_kernel(
@@ -39,21 +42,27 @@ def tile_picked_zsmoe_relu_po_kernel(
 ):
     nc = tc.nc
     weights = (w1, w2)
-    pieces = [(h, d, a) for h in range(HALVES) for d in range(LAYERS) for a in range(PASSES)]
+    steps = [(h, d) for h in range(HALVES) for d in range(LAYERS)]
+    pieces = [step + (a,) for step in steps for a in range(PASSES)]
 
     with ExitStack() as ctx:
         keep = ctx.enter_context(tc.tile_pool(name="keep", bufs=1))
-        late = ctx.enter_context(tc.tile_pool(name="late", bufs=1))
+        placed = ctx.enter_context(tc.tile_pool(name="placed", bufs=1))
         psum = ctx.enter_context(tc.psum_pool(name="psum", bufs=1))
 
-        def tile(shape, dtype, name):
-            return keep.tile(shape, dtype, name=name, align_bytes=64)
+        def tile(shape, dtype, name, tag=None):
+            return keep.tile(shape, dtype, name=name, tag=tag or name, align_bytes=64)
 
-        offsets = keep.tile([P, S // 16], U16, name="offsets")
+        def placed_tile(shape, name, offset):
+            return placed.tile(shape, F32, name=name, offset=offset, align_bytes=64)
+
+        def bank(name, shape):
+            return psum.tile(shape, F32, name=name, tag=name)
+
+        offsets = keep.tile([P, S // LIST_ROWS], U16, name="offsets")
         word_table = [tile([P, T], U32, "word_table%d" % a) for a in range(PASSES)]
         scale_table = tile([P, T], U8, "scale_table")
         gate_table = tile([P, T], F32, "gate_table")
-        raw = {}
         rounded = {q: tile([P, HALF, PACK], BF16, "rounded%d%d%d" % q) for q in pieces}
         w_words = {q: tile([P, HALF], U32, "w_words%d%d%d" % q) for q in pieces}
         w_scales = {q: tile([P, HALF], U8, "w_scales%d%d%d" % q) for q in pieces}
@@ -61,44 +70,33 @@ def tile_picked_zsmoe_relu_po_kernel(
         picked_scales = tile([P, S], U8, "picked_scales")
         picked_gate = tile([P, S], F32, "picked_gate")
         identity = tile([P, P], F32, "identity")
-        gated = {}
-        y = {}
-        y_rounded = {}
-        y_words = [tile([P, BANKS * P], U32, "y_words%d" % h) for h in range(HALVES)]
-        y_scales = tile([P, HALVES, BANKS * P], U8, "y_scales")
-
-        def bank(name, shape):
-            return psum.tile(shape, F32, name=name, tag=name)
+        y_rounded = [tile([P, PAIRS * P, PACK], BF16, "y_rounded%d" % h) for h in range(HALVES)]
+        y_words = [tile([P, PAIRS * P], U32, "y_words%d" % h) for h in range(HALVES)]
+        y_scales = tile([P, HALVES, PAIRS * P], U8, "y_scales")
+        raw, products, gated, sums, y = {}, {}, {}, {}, {}
 
         def load_words(a):
             nc.sync.dma_start(
                 out=word_table[a][:].bitcast(I32), in_=x_words[a].rearrange("p c r -> p (c r)").bitcast(I32)
             )
 
-        def load_half(h, d, a):
+        def load_weights(q):
+            h, d, a = q
             rows = weights[d][a * P * PACK : (a + 1) * P * PACK, h * HALF : (h + 1) * HALF]
-            if (h, d, a) == pieces[-1]:
-                piece = late.tile([P, PACK, HALF], F32, name="raw_last", offset=0, align_bytes=64)
+            if q == pieces[-1]:
+                raw[q] = placed_tile([P, PACK, HALF], "raw_last", 0)
             else:
-                piece = tile([P, PACK, HALF], F32, "raw%d%d%d" % (h, d, a))
-            nc.sync.dma_start(out=piece[:], in_=rows.rearrange("(p j) c -> p j c", j=PACK))
-            raw[h, d, a] = piece[:]
-
-        def load_pass(d, a):
-            rows = weights[d][a * P * PACK : (a + 1) * P * PACK, :]
-            piece = tile([P, PACK, N], F32, "whole%d%d" % (d, a))
-            nc.sync.dma_start(out=piece[:], in_=rows.rearrange("(p j) c -> p j c", j=PACK))
-            for h in range(HALVES):
-                raw[h, d, a] = piece[:, :, h * HALF : (h + 1) * HALF]
+                raw[q] = tile([P, PACK, HALF], F32, "raw%d%d%d" % q)
+            nc.sync.dma_start(out=raw[q][:], in_=rows.rearrange("(p j) c -> p j c", j=PACK))
 
         def interleave(copy, dst, src):
             copy(dst.rearrange("p (c i) j -> p c j i", i=2), src.rearrange("p j (c i) -> p c j i", i=2))
 
-        def round_weights(q):
-            vector_from = HALF - VECTOR_COLUMNS[pieces.index(q)]
-            interleave(nc.scalar.copy, rounded[q][:, :vector_from, :], raw[q][:, :, :vector_from])
-            if vector_from < HALF:
-                interleave(nc.vector.tensor_copy, rounded[q][:, vector_from:, :], raw[q][:, :, vector_from:])
+        def round_weights(q, vector_columns=0):
+            split = HALF - vector_columns
+            interleave(nc.scalar.copy, rounded[q][:, :split, :], raw[q][:, :, :split])
+            if vector_columns:
+                interleave(nc.vector.tensor_copy, rounded[q][:, split:, :], raw[q][:, :, split:])
 
         def quantize_weights(q):
             nc.vector.quantize_mx(
@@ -107,120 +105,102 @@ def tile_picked_zsmoe_relu_po_kernel(
                 in_=rounded[q][:].rearrange("p c j -> p (c j)"),
             )
 
-        products = {}
-
-        def multiply(q, banks):
+        def multiply(q, pair):
             h, d, a = q
-            for u in banks:
-                for side in range(SIDES):
-                    b = SIDES * side + u
-                    if a == 0:
-                        products[h, d, b] = bank("product%d" % b, [P, HALF])
-                    tokens = slice(b * P, (b + 1) * P)
-                    nc.tensor.matmul_mx(
-                        out=products[h, d, b][:],
-                        lhsT=picked_words[a][:, tokens].bitcast(FP8X4),
-                        lhsT_scale=picked_scales[4 * a : P, tokens],
-                        rhs=w_words[q][:].bitcast(FP8X4),
-                        rhs_scale=w_scales[q][:],
-                        start=(a == 0),
-                        stop=(a == PASSES - 1),
-                    )
+            for side in range(SIDES):
+                b = PAIRS * side + pair
+                if a == 0:
+                    products[h, d, b] = bank("product%d" % b, [P, HALF])
+                tokens = slice(b * P, (b + 1) * P)
+                nc.tensor.matmul_mx(
+                    out=products[h, d, b][:],
+                    lhsT=picked_words[a][:, tokens].bitcast(FP8X4),
+                    lhsT_scale=picked_scales[SCALE_ROWS * a : P, tokens],
+                    rhs=w_words[q][:].bitcast(FP8X4),
+                    rhs_scale=w_scales[q][:],
+                    start=(a == 0),
+                    stop=(a == PASSES - 1),
+                )
 
-        sums = {}
+        def apply_gate(step, pair, into):
+            h, d = step
+            gated[h, d, pair] = into
+            for side in range(SIDES):
+                b = PAIRS * side + pair
+                nc.vector.tensor_scalar(
+                    out=into[:, :, side, :],
+                    in0=products[h, d, b][:].rearrange("p (i t) -> p t i", t=PACK),
+                    scalar1=0.0,
+                    scalar2=token_gate[:, b, d : d + 1],
+                    op0=MAX,
+                    op1=MULT,
+                )
 
-        def apply_gate(h, d, u, tag):
-            if tag == "raw111":
-                gated[h, d, u] = late.tile([P, PACK, SIDES, WORDS], F32, name="gated101", offset=0, align_bytes=64)
-            else:
-                gated[h, d, u] = keep.tile([P, PACK, SIDES, WORDS], F32, name="gated%d%d%d" % (h, d, u), tag=tag, align_bytes=64)
-            if True:
-                for side in range(SIDES):
-                    b = SIDES * side + u
-                    dealt = products[h, d, b][:].rearrange("p (i t) -> p t i", t=PACK)
-                    dst = gated[h, d, u][:, :, side, :]
-                    factor = token_gate[:, b, d : d + 1]
-                    if (h, d, b) in SCALAR_GATED:
-                        positive = tile([P, PACK, WORDS], F32, "positive%d%d%d" % (h, d, b))
-                        nc.scalar.activation(out=positive[:], in_=dealt, func=RELU)
-                        nc.scalar.activation(out=dst, in_=positive[:], func=COPY, scale=factor)
-                    else:
-                        nc.vector.tensor_scalar(out=dst, in0=dealt, scalar1=0.0, scalar2=factor, op0=MAX, op1=MULT)
-
-        def turn(h, d, u):
+        def turn(step, pair):
+            h, d = step
             if d == 0:
-                if (h, u) == (HALVES - 1, BANKS - 1):
-                    sums[h, u] = [bank(name, [P, 2, P]) for name in ("sum3", "sum0")]
+                if (h, pair) == (HALVES - 1, PAIRS - 1):
+                    sums[h, pair] = [bank(name, [P, PACK // 2, P]) for name in ("sum3", "sum0")]
                 else:
-                    sums[h, u] = [bank("sum%d" % (BANKS * h + u), [P, PACK, P])]
-            share = PACK // len(sums[h, u])
+                    sums[h, pair] = [bank("sum%d" % (PAIRS * h + pair), [P, PACK, P])]
+            share = PACK // len(sums[h, pair])
             for t in range(PACK):
                 nc.tensor.matmul(
-                    out=sums[h, u][t // share][:, t % share, :],
-                    lhsT=gated[h, d, u][:, t, :, :].rearrange("p s i -> p (s i)"),
+                    out=sums[h, pair][t // share][:, t % share, :],
+                    lhsT=gated[h, d, pair][:, t, :, :].rearrange("p s i -> p (s i)"),
                     rhs=identity[:],
                     is_transpose=True,
                     start=(d == 0 and t % share == 0),
                     stop=(d == LAYERS - 1 and t % share == share - 1),
                 )
 
-        def copy_sum(copy, h, u, part=0):
-            if h not in y:
-                y[h] = late.tile([P, PACK, BANKS, P], F32, name="y%d" % h, offset=2048 + 4096 * h, align_bytes=64)
-            share = PACK // len(sums[h, u])
-            copy(y[h][:, part * share : (part + 1) * share, u, :], sums[h, u][part][:])
+        def copy_sum(copy, h, pair, part=0):
+            share = PACK // len(sums[h, pair])
+            copy(y[h][:, part * share : (part + 1) * share, pair, :], sums[h, pair][part][:])
 
-        def rounded_sum(h, u):
-            if h not in y_rounded:
-                y_rounded[h] = keep.tile([P, BANKS * P, PACK], BF16, name="y_rounded%d" % h, tag="y_rounded%d" % h, align_bytes=64)
-            return y_rounded[h][:, u * P : (u + 1) * P, :]
+        def round_sum(copy, h, pair):
+            interleave(copy, y_rounded[h][:, pair * P : (pair + 1) * P, :], y[h][:, :, pair, :])
 
-        def round_from_copy(copy, h, u):
-            interleave(copy, rounded_sum(h, u), y[h][:, :, u, :])
-
-        def quantize_sum(h, u0, u1):
+        def quantize_sum(h):
             nc.vector.quantize_mx(
-                out=y_words[h][:, u0 * P : u1 * P].bitcast(FP8X4),
-                scales=y_scales[:, h, u0 * P : u1 * P],
-                in_=y_rounded[h][:, u0 * P : u1 * P, :].rearrange("p c t -> p (c t)"),
+                out=y_words[h][:].bitcast(FP8X4),
+                scales=y_scales[:, h, :],
+                in_=y_rounded[h][:].rearrange("p c t -> p (c t)"),
             )
+
+        def side_of(side):
+            return slice(side * WORDS, (side + 1) * WORDS), slice(side * PAIRS * P, (side + 1) * PAIRS * P)
 
         def store_values(h):
             rows = out_0[h * HALF : (h + 1) * HALF, :].rearrange("(i t) c -> i t c", t=PACK)
-            for side in range(SIDES):
-                held = slice(side * WORDS, (side + 1) * WORDS)
-                tokens = slice(side * BANKS * P, (side + 1) * BANKS * P)
-                queue = nc.scalar if side else nc.sync
+            for side, queue in enumerate((nc.sync, nc.scalar)):
+                held, tokens = side_of(side)
                 queue.dma_start(out=rows[:, :, tokens], in_=y[h][held].rearrange("p t u j -> p t (u j)"))
 
-        def store_words(h):
+        def store_words(h, queues):
             words = out_1[0, h * WORDS : (h + 1) * WORDS].rearrange("i c r -> i (c r)").bitcast(I32)
-            for side in range(SIDES):
-                held = slice(side * WORDS, (side + 1) * WORDS)
-                tokens = slice(side * BANKS * P, (side + 1) * BANKS * P)
-                queue = nc.scalar if side and h else nc.sync
+            for side, queue in enumerate(queues):
+                held, tokens = side_of(side)
                 queue.dma_start(out=words[:, tokens], in_=y_words[h][held].bitcast(I32))
 
-        warm = tile([P, 16], F32, "warm")
-        nc.vector.memset(warm[:, 0:8], 0.0)
-        nc.scalar.copy(warm[:, 8:16], warm[:, 0:8])
         nc.vector.memset(scale_table[:].bitcast(I32), 0)
         nc.vector.memset(gate_table[:].bitcast(I32), 0)
         nc.vector.memset(identity[:], 0.0)
         make_identity(nc, identity[:], nomemset=True)
+
         load_words(0)
         nc.sync.dma_start(offsets[:], offs)
-        for quad in range(4):
+        for quad in range(P // QUADRANT):
             nc.sync.dma_start(
-                out=scale_table[32 * quad : 32 * quad + 4 * PASSES, :].bitcast(I32),
-                in_=x_scales[:, 4 * quad : 4 * quad + 4, :].bitcast(I32),
+                out=scale_table[QUADRANT * quad : QUADRANT * quad + SCALE_ROWS * PASSES, :].bitcast(I32),
+                in_=x_scales[:, SCALE_ROWS * quad : SCALE_ROWS * (quad + 1), :].bitcast(I32),
             )
         nc.sync.dma_start(out=gate_table[0:LAYERS, :], in_=gate[:, 0, :])
-        load_half(*pieces[0])
-        load_half(*pieces[1])
+        load_weights(pieces[0])
+        load_weights(pieces[1])
         load_words(1)
-        for q in pieces[2:]:
-            load_half(*q)
+        for q in pieces[PASSES:]:
+            load_weights(q)
 
         nc.vector.tensor_copy(picked_words[0][:], word_table[0][:].indirect(offsets[:]))
         nc.vector.tensor_copy(picked_scales[:], scale_table[:].indirect(offsets[:]))
@@ -230,61 +210,71 @@ def tile_picked_zsmoe_relu_po_kernel(
             nc.tensor.transpose(turned_gate[:, b, :], picked_gate[:, b * P : (b + 1) * P], identity[:])
         round_weights(pieces[0])
         quantize_weights(pieces[0])
-        multiply(pieces[0], (0, 1))
-        picked_words.append(tile([P, S], U32, "picked_words1"))
+        for pair in range(PAIRS):
+            multiply(pieces[0], pair)
+        picked_words.append(tile([P, S], U32, "picked_words1", "rounded000"))
         round_weights(pieces[1])
-        token_gate = keep.tile([P, BLOCKS, LAYERS], F32, name="token_gate", tag="raw001", align_bytes=64)
-        nc.scalar.copy(token_gate[:], turned_gate[:, :, 0:LAYERS])
-        for u in range(BANKS):
+        for pair in range(PAIRS):
             for side in range(SIDES):
-                b = BANKS * side + u
+                b = PAIRS * side + pair
                 nc.vector.tensor_copy(
                     picked_words[1][:, b * P : (b + 1) * P],
-                    word_table[1][:].indirect(offsets[:, b * P // 16 : (b + 1) * P // 16]),
+                    word_table[1][:].indirect(offsets[:, b * P // LIST_ROWS : (b + 1) * P // LIST_ROWS]),
                 )
-            if u == 0:
+            if pair == 0:
                 quantize_weights(pieces[1])
-            multiply(pieces[1], (u,))
+            multiply(pieces[1], pair)
+        token_gate = tile([P, BLOCKS, LAYERS], F32, "token_gate", "rounded001")
+        nc.vector.tensor_copy(token_gate[:], turned_gate[:, :, 0:LAYERS])
 
-        steps = [(h, d) for h in range(HALVES) for d in range(LAYERS)]
+        gated_shape = [P, PACK, SIDES, WORDS]
         for n, step in enumerate(steps):
-            last = n == len(steps) - 1
-            apply_gate(*step, 0, "gated%d%d0" % step)
+            apply_gate(step, 0, tile(gated_shape, F32, "gated%d%d0" % step))
             if n > 0:
-                turn(*steps[n - 1], 1)
-            turn(*step, 0)
-            if not last:
-                nxt = steps[n + 1]
-                for a in range(PASSES):
-                    round_weights(nxt + (a,))
-                    quantize_weights(nxt + (a,))
-                    multiply(nxt + (a,), (0,))
-            apply_gate(*step, 1, "gated%d%d1" % step if last else "raw%d%d1" % nxt)
-            if not last:
-                for a in range(PASSES):
-                    multiply(nxt + (a,), (1,))
-        turn(*steps[-1], 1)
-        for u in range(BANKS):
-            copy_sum(nc.scalar.copy, 0, u)
-        for u in range(BANKS):
-            round_from_copy(nc.scalar.copy, 0, u)
+                turn(steps[n - 1], 1)
+            turn(step, 0)
+            if step == steps[-1]:
+                apply_gate(step, 1, tile(gated_shape, F32, "gated%d%d1" % step))
+                turn(step, 1)
+                break
+            first, second = pieces[PASSES * (n + 1) : PASSES * (n + 2)]
+            round_weights(first)
+            quantize_weights(first)
+            multiply(first, 0)
+            round_weights(second, VECTOR_COLUMNS_LAST if second == pieces[-1] else VECTOR_COLUMNS)
+            quantize_weights(second)
+            multiply(second, 0)
+            if second == pieces[-1]:
+                apply_gate(step, 1, placed_tile(gated_shape, "gated_on_raw_last", 0))
+            else:
+                apply_gate(step, 1, tile(gated_shape, F32, "gated%d%d1" % step, "raw%d%d%d" % second))
+            multiply(first, 1)
+            multiply(second, 1)
+
+        y[0] = placed_tile([P, PACK, PAIRS, P], "y0", GATED_BYTES)
+        for pair in range(PAIRS):
+            copy_sum(nc.scalar.copy, 0, pair)
+        for pair in range(PAIRS):
+            round_sum(nc.scalar.copy, 0, pair)
         store_values(0)
-        quantize_sum(0, 0, BANKS)
-        store_words(0)
+        quantize_sum(0)
+        store_words(0, (nc.sync, nc.sync))
+
+        y[1] = placed_tile([P, PACK, PAIRS, P], "y1", GATED_BYTES + Y_BYTES)
         copy_sum(nc.scalar.copy, 1, 0)
         copy_sum(nc.vector.tensor_copy, 1, 1, 0)
         copy_sum(nc.scalar.copy, 1, 1, 1)
         store_values(1)
-        round_from_copy(nc.vector.tensor_copy, 1, 0)
-        round_from_copy(nc.vector.tensor_copy, 1, 1)
-        quantize_sum(1, 0, BANKS)
-        store_words(1)
-        scale_rows = out_2[0].rearrange("(h g r) c -> g r h c", h=HALVES, r=4)
-        for quad in range(4):
+        for pair in range(PAIRS):
+            round_sum(nc.vector.tensor_copy, 1, pair)
+        quantize_sum(1)
+        store_words(1, (nc.sync, nc.scalar))
+
+        scale_rows = out_2[0].rearrange("(h g r) c -> g r h c", h=HALVES, r=SCALE_ROWS)
+        for quad in range(P // QUADRANT):
             side, group = divmod(quad, 2)
-            tokens = slice(side * BANKS * P, (side + 1) * BANKS * P)
-            queue = nc.scalar if quad % 2 else nc.sync
+            queue = nc.scalar if group else nc.sync
             queue.dma_start(
-                out=scale_rows[group][:, :, tokens].bitcast(I32),
-                in_=y_scales[32 * quad : 32 * quad + 4].bitcast(I32),
+                out=scale_rows[group][:, :, side_of(side)[1]].bitcast(I32),
+                in_=y_scales[QUADRANT * quad : QUADRANT * quad + SCALE_ROWS].bitcast(I32),
             )

@@ -66,14 +66,14 @@ def tile_picked_zsmoe_relu_po_kernel(
         rounded = {q: tile([P, HALF, PACK], BF16, "rounded%d%d%d" % q) for q in pieces}
         w_words = {q: tile([P, HALF], U32, "w_words%d%d%d" % q) for q in pieces}
         w_scales = {q: tile([P, HALF], U8, "w_scales%d%d%d" % q) for q in pieces}
-        picked_words = [tile([P, S], U32, "picked_words0")]
+        picked_first = tile([P, S], U32, "picked_first")
         picked_scales = tile([P, S], U8, "picked_scales")
         picked_gate = tile([P, S], F32, "picked_gate")
         identity = tile([P, P], F32, "identity")
         y_rounded = [tile([P, PAIRS * P, PACK], BF16, "y_rounded%d" % h) for h in range(HALVES)]
         y_words = [tile([P, PAIRS * P], U32, "y_words%d" % h) for h in range(HALVES)]
         y_scales = tile([P, HALVES, PAIRS * P], U8, "y_scales")
-        raw, products, gated, sums, y = {}, {}, {}, {}, {}
+        raw, picked_words, products, gated, sums, y = {}, {}, {}, {}, {}, {}
 
         def load_words(a):
             nc.sync.dma_start(
@@ -114,7 +114,7 @@ def tile_picked_zsmoe_relu_po_kernel(
                 tokens = slice(b * P, (b + 1) * P)
                 nc.tensor.matmul_mx(
                     out=products[h, d, b][:],
-                    lhsT=picked_words[a][:, tokens].bitcast(FP8X4),
+                    lhsT=picked_words[a, b].bitcast(FP8X4),
                     lhsT_scale=picked_scales[SCALE_ROWS * a : P, tokens],
                     rhs=w_words[q][:].bitcast(FP8X4),
                     rhs_scale=w_scales[q][:],
@@ -202,7 +202,9 @@ def tile_picked_zsmoe_relu_po_kernel(
         for q in pieces[PASSES:]:
             load_weights(q)
 
-        nc.vector.tensor_copy(picked_words[0][:], word_table[0][:].indirect(offsets[:]))
+        nc.vector.tensor_copy(picked_first[:], word_table[0][:].indirect(offsets[:]))
+        for b in range(BLOCKS):
+            picked_words[0, b] = picked_first[:, b * P : (b + 1) * P]
         nc.vector.tensor_copy(picked_scales[:], scale_table[:].indirect(offsets[:]))
         nc.vector.tensor_copy(picked_gate[:], gate_table[:].indirect(offsets[:]))
         turned_gate = bank("sum0", [P, BLOCKS, P])
@@ -212,20 +214,21 @@ def tile_picked_zsmoe_relu_po_kernel(
         quantize_weights(pieces[0])
         for pair in range(PAIRS):
             multiply(pieces[0], pair)
-        picked_words.append(tile([P, S], U32, "picked_words1", "rounded000"))
         round_weights(pieces[1])
         for pair in range(PAIRS):
+            picked_pair = tile([P, SIDES, P], U32, "picked_second%d" % pair, "rounded00%d" % pair)
             for side in range(SIDES):
                 b = PAIRS * side + pair
+                picked_words[1, b] = picked_pair[:, side, :]
                 nc.vector.tensor_copy(
-                    picked_words[1][:, b * P : (b + 1) * P],
+                    picked_words[1, b],
                     word_table[1][:].indirect(offsets[:, b * P // LIST_ROWS : (b + 1) * P // LIST_ROWS]),
                 )
             if pair == 0:
                 quantize_weights(pieces[1])
+                token_gate = tile([P, BLOCKS, LAYERS], F32, "token_gate", "raw001")
+                nc.vector.tensor_copy(token_gate[:], turned_gate[:, :, 0:LAYERS])
             multiply(pieces[1], pair)
-        token_gate = tile([P, BLOCKS, LAYERS], F32, "token_gate", "rounded001")
-        nc.vector.tensor_copy(token_gate[:], turned_gate[:, :, 0:LAYERS])
 
         gated_shape = [P, PACK, SIDES, WORDS]
         for n, step in enumerate(steps):
@@ -239,11 +242,10 @@ def tile_picked_zsmoe_relu_po_kernel(
                 break
             first, second = pieces[PASSES * (n + 1) : PASSES * (n + 2)]
             round_weights(first)
-            quantize_weights(first)
-            multiply(first, 0)
             round_weights(second, VECTOR_COLUMNS_LAST if second == pieces[-1] else VECTOR_COLUMNS)
-            quantize_weights(second)
-            multiply(second, 0)
+            for q in (first, second):
+                quantize_weights(q)
+                multiply(q, 0)
             if second == pieces[-1]:
                 apply_gate(step, 1, placed_tile(gated_shape, "gated_on_raw_last", 0))
             else:

@@ -31,8 +31,8 @@ FP8X4 = mybir.dt.float8_e4m3fn_x4
 MAX = mybir.AluOpType.max
 MULT = mybir.AluOpType.mult
 
-VECTOR_COLUMNS = 96
-VECTOR_COLUMNS_LAST = 128
+VECTOR_COLUMNS = 128
+VECTOR_COLUMNS_LAST = 144
 GATED_BYTES = PACK * P * 4
 Y_BYTES = PAIRS * GATED_BYTES
 

@@ -183,30 +183,30 @@ def tile_picked_zsmoe_relu_po_kernel(
                 held, tokens = side_of(side)
                 queue.dma_start(out=words[:, tokens], in_=y_words[h][held].bitcast(I32))
 
-        nc.vector.memset(scale_table[:].bitcast(I32), 0)
         nc.vector.memset(gate_table[:].bitcast(I32), 0)
+        nc.vector.memset(scale_table[:].bitcast(I32), 0)
         nc.vector.memset(identity[:], 0.0)
         make_identity(nc, identity[:], nomemset=True)
 
-        load_words(0)
         nc.sync.dma_start(offsets[:], offs)
+        nc.scalar.dma_start(out=gate_table[0:LAYERS, :], in_=gate[:, 0, :])
+        load_words(0)
         for quad in range(P // QUADRANT):
             nc.sync.dma_start(
                 out=scale_table[QUADRANT * quad : QUADRANT * quad + SCALE_ROWS * PASSES, :].bitcast(I32),
                 in_=x_scales[:, SCALE_ROWS * quad : SCALE_ROWS * (quad + 1), :].bitcast(I32),
             )
-        nc.sync.dma_start(out=gate_table[0:LAYERS, :], in_=gate[:, 0, :])
         load_weights(pieces[0])
         load_weights(pieces[1])
         load_words(1)
         for q in pieces[PASSES:]:
             load_weights(q)
 
+        nc.vector.tensor_copy(picked_gate[:], gate_table[:].indirect(offsets[:]))
         nc.vector.tensor_copy(picked_first[:], word_table[0][:].indirect(offsets[:]))
         for b in range(BLOCKS):
             picked_words[0, b] = picked_first[:, b * P : (b + 1) * P]
         nc.vector.tensor_copy(picked_scales[:], scale_table[:].indirect(offsets[:]))
-        nc.vector.tensor_copy(picked_gate[:], gate_table[:].indirect(offsets[:]))
         turned_gate = bank("sum0", [P, BLOCKS, P])
         for b in range(BLOCKS):
             nc.tensor.transpose(turned_gate[:, b, :], picked_gate[:, b * P : (b + 1) * P], identity[:])

@@ -188,9 +188,9 @@ def tile_picked_zsmoe_relu_po_kernel(
         nc.vector.memset(identity[:], 0.0)
         make_identity(nc, identity[:], nomemset=True)
 
+        load_words(0)
         nc.sync.dma_start(offsets[:], offs)
         nc.scalar.dma_start(out=gate_table[0:LAYERS, :], in_=gate[:, 0, :])
-        load_words(0)
         for quad in range(P // QUADRANT):
             nc.sync.dma_start(
                 out=scale_table[QUADRANT * quad : QUADRANT * quad + SCALE_ROWS * PASSES, :].bitcast(I32),

@@ -171,9 +171,9 @@ def tile_picked_zsmoe_relu_po_kernel(
         def side_of(side):
             return slice(side * WORDS, (side + 1) * WORDS), slice(side * PAIRS * P, (side + 1) * PAIRS * P)
 
-        def store_values(h):
+        def store_values(h, queues):
             rows = out_0[h * HALF : (h + 1) * HALF, :].rearrange("(i t) c -> i t c", t=PACK)
-            for side, queue in enumerate((nc.sync, nc.scalar)):
+            for side, queue in enumerate(queues):
                 held, tokens = side_of(side)
                 queue.dma_start(out=rows[:, :, tokens], in_=y[h][held].rearrange("p t u j -> p t (u j)"))
 
@@ -258,7 +258,7 @@ def tile_picked_zsmoe_relu_po_kernel(
             copy_sum(nc.scalar.copy, 0, pair)
         for pair in range(PAIRS):
             round_sum(nc.scalar.copy, 0, pair)
-        store_values(0)
+        store_values(0, (nc.sync, nc.scalar))
         quantize_sum(0)
         store_words(0, (nc.sync, nc.sync))
 
@@ -266,11 +266,11 @@ def tile_picked_zsmoe_relu_po_kernel(
         copy_sum(nc.scalar.copy, 1, 0)
         copy_sum(nc.vector.tensor_copy, 1, 1, 0)
         copy_sum(nc.scalar.copy, 1, 1, 1)
-        store_values(1)
+        store_values(1, (nc.sync, nc.sync))
         for pair in range(PAIRS):
             round_sum(nc.vector.tensor_copy, 1, pair)
         quantize_sum(1)
-        store_words(1, (nc.sync, nc.scalar))
+        store_words(1, (nc.sync, nc.sync))
 
         scale_rows = out_2[0].rearrange("(h g r) c -> g r h c", h=HALVES, r=SCALE_ROWS)
         for quad in range(P // QUADRANT):

@@ -253,12 +253,12 @@ def tile_picked_zsmoe_relu_po_kernel(
             multiply(first, 1)
             multiply(second, 1)
 
-        y[0] = placed_tile([P, PACK, PAIRS, P], "y0", GATED_BYTES)
+        y[0] = tile([P, PACK, PAIRS, P], F32, "y0", "raw%d%d%d" % pieces[-2])
         for pair in range(PAIRS):
             copy_sum(nc.scalar.copy, 0, pair)
         for pair in range(PAIRS):
             round_sum(nc.scalar.copy, 0, pair)
-        store_values(0, (nc.sync, nc.scalar))
+        store_values(0, (nc.sync, nc.sync))
         quantize_sum(0)
         store_words(0, (nc.sync, nc.sync))
 

@@ -30,7 +30,9 @@ U8 = mybir.dt.uint8
 FP8X4 = mybir.dt.float8_e4m3fn_x4
 MAX = mybir.AluOpType.max
 MULT = mybir.AluOpType.mult
+COPY = mybir.ActivationFunctionType.Copy
 
+VECTOR_COLUMNS_FIRST = (128, 176)
 VECTOR_COLUMNS = 128
 VECTOR_COLUMNS_LAST = 144
 GATED_BYTES = PACK * P * 4
@@ -105,11 +107,12 @@ def tile_picked_zsmoe_relu_po_kernel(
                 in_=rounded[q][:].rearrange("p c j -> p (c j)"),
             )
 
-        def multiply(q, pair):
+        def multiply(q, pair, opens=None):
             h, d, a = q
+            opens = a == 0 if opens is None else opens
             for side in range(SIDES):
                 b = PAIRS * side + pair
-                if a == 0:
+                if opens:
                     products[h, d, b] = bank("product%d" % b, [P, HALF])
                 tokens = slice(b * P, (b + 1) * P)
                 nc.tensor.matmul_mx(
@@ -118,8 +121,8 @@ def tile_picked_zsmoe_relu_po_kernel(
                     lhsT_scale=picked_scales[SCALE_ROWS * a : P, tokens],
                     rhs=w_words[q][:].bitcast(FP8X4),
                     rhs_scale=w_scales[q][:],
-                    start=(a == 0),
-                    stop=(a == PASSES - 1),
+                    start=opens,
+                    stop=not opens,
                 )
 
         def apply_gate(step, pair, into):
@@ -185,12 +188,12 @@ def tile_picked_zsmoe_relu_po_kernel(
 
         nc.vector.memset(gate_table[:].bitcast(I32), 0)
         nc.vector.memset(scale_table[:].bitcast(I32), 0)
-        nc.vector.memset(identity[:], 0.0)
+        nc.any.memset(identity[:], 0.0)
         make_identity(nc, identity[:], nomemset=True)
 
         load_words(0)
         nc.sync.dma_start(offsets[:], offs)
-        nc.scalar.dma_start(out=gate_table[0:LAYERS, :], in_=gate[:, 0, :])
+        nc.sync.dma_start(out=gate_table[0:LAYERS, :], in_=gate[:, 0, :])
         for quad in range(P // QUADRANT):
             nc.sync.dma_start(
                 out=scale_table[QUADRANT * quad : QUADRANT * quad + SCALE_ROWS * PASSES, :].bitcast(I32),
@@ -202,7 +205,7 @@ def tile_picked_zsmoe_relu_po_kernel(
         for q in pieces[PASSES:]:
             load_weights(q)
 
-        nc.vector.tensor_copy(picked_gate[:], gate_table[:].indirect(offsets[:]))
+        nc.scalar.activation(picked_gate[:], gate_table[:].indirect(offsets[:]), COPY)
         nc.vector.tensor_copy(picked_first[:], word_table[0][:].indirect(offsets[:]))
         for b in range(BLOCKS):
             picked_words[0, b] = picked_first[:, b * P : (b + 1) * P]
@@ -210,25 +213,24 @@ def tile_picked_zsmoe_relu_po_kernel(
         turned_gate = bank("sum0", [P, BLOCKS, P])
         for b in range(BLOCKS):
             nc.tensor.transpose(turned_gate[:, b, :], picked_gate[:, b * P : (b + 1) * P], identity[:])
-        round_weights(pieces[0])
+        round_weights(pieces[0], VECTOR_COLUMNS_FIRST[0])
         quantize_weights(pieces[0])
+        multiply(pieces[0], 0)
+        round_weights(pieces[1], VECTOR_COLUMNS_FIRST[1])
+        quantize_weights(pieces[1])
+        token_gate = tile([P, BLOCKS, LAYERS], F32, "token_gate", "raw001")
+        nc.scalar.copy(token_gate[:], turned_gate[:, :, 0:LAYERS])
+        picked_second = tile([P, BLOCKS, P], U32, "picked_second")
         for pair in range(PAIRS):
-            multiply(pieces[0], pair)
-        round_weights(pieces[1])
-        for pair in range(PAIRS):
-            picked_pair = tile([P, SIDES, P], U32, "picked_second%d" % pair, "rounded00%d" % pair)
             for side in range(SIDES):
                 b = PAIRS * side + pair
-                picked_words[1, b] = picked_pair[:, side, :]
+                picked_words[1, b] = picked_second[:, b, :]
                 nc.vector.tensor_copy(
                     picked_words[1, b],
                     word_table[1][:].indirect(offsets[:, b * P // LIST_ROWS : (b + 1) * P // LIST_ROWS]),
                 )
-            if pair == 0:
-                quantize_weights(pieces[1])
-                token_gate = tile([P, BLOCKS, LAYERS], F32, "token_gate", "raw001")
-                nc.vector.tensor_copy(token_gate[:], turned_gate[:, :, 0:LAYERS])
-            multiply(pieces[1], pair)
+            multiply(pieces[1], pair, pair == 1)
+        multiply(pieces[0], 1, False)
 
         gated_shape = [P, PACK, SIDES, WORDS]
         for n, step in enumerate(steps):
@@ -253,12 +255,12 @@ def tile_picked_zsmoe_relu_po_kernel(
             multiply(first, 1)
             multiply(second, 1)
 
-        y[0] = tile([P, PACK, PAIRS, P], F32, "y0", "raw%d%d%d" % pieces[-2])
+        y[0] = placed_tile([P, PACK, PAIRS, P], "y0", GATED_BYTES)
         for pair in range(PAIRS):
             copy_sum(nc.scalar.copy, 0, pair)
         for pair in range(PAIRS):
             round_sum(nc.scalar.copy, 0, pair)
-        store_values(0, (nc.sync, nc.sync))
+        store_values(0, (nc.sync, nc.scalar))
         quantize_sum(0)
         store_words(0, (nc.sync, nc.sync))
 

@@ -53,10 +53,10 @@ def tile_picked_zsmoe_relu_po_kernel(
         psum = ctx.enter_context(tc.psum_pool(name="psum", bufs=1))
 
         def tile(shape, dtype, name, tag=None):
-            return keep.tile(shape, dtype, name=name, tag=tag or name, align_bytes=64)
+            return keep.tile(shape, dtype, name=name, tag=tag or name, align_bytes=256)
 
         def placed_tile(shape, name, offset):
-            return placed.tile(shape, F32, name=name, offset=offset, align_bytes=64)
+            return placed.tile(shape, F32, name=name, offset=offset, align_bytes=256)
 
         def bank(name, shape):
             return psum.tile(shape, F32, name=name, tag=name)

@@ -174,17 +174,17 @@ def tile_picked_zsmoe_relu_po_kernel(
         def side_of(side):
             return slice(side * WORDS, (side + 1) * WORDS), slice(side * PAIRS * P, (side + 1) * PAIRS * P)
 
-        def store_values(h, queues):
+        def store_values(h):
             rows = out_0[h * HALF : (h + 1) * HALF, :].rearrange("(i t) c -> i t c", t=PACK)
-            for side, queue in enumerate(queues):
+            for side in range(SIDES):
                 held, tokens = side_of(side)
-                queue.dma_start(out=rows[:, :, tokens], in_=y[h][held].rearrange("p t u j -> p t (u j)"))
+                nc.sync.dma_start(out=rows[:, :, tokens], in_=y[h][held].rearrange("p t u j -> p t (u j)"))
 
-        def store_words(h, queues):
+        def store_words(h):
             words = out_1[0, h * WORDS : (h + 1) * WORDS].rearrange("i c r -> i (c r)").bitcast(I32)
-            for side, queue in enumerate(queues):
+            for side in range(SIDES):
                 held, tokens = side_of(side)
-                queue.dma_start(out=words[:, tokens], in_=y_words[h][held].bitcast(I32))
+                nc.sync.dma_start(out=words[:, tokens], in_=y_words[h][held].bitcast(I32))
 
         nc.vector.memset(gate_table[:].bitcast(I32), 0)
         nc.vector.memset(scale_table[:].bitcast(I32), 0)
@@ -260,19 +260,19 @@ def tile_picked_zsmoe_relu_po_kernel(
             copy_sum(nc.scalar.copy, 0, pair)
         for pair in range(PAIRS):
             round_sum(nc.scalar.copy, 0, pair)
-        store_values(0, (nc.sync, nc.scalar))
+        store_values(0)
         quantize_sum(0)
-        store_words(0, (nc.sync, nc.sync))
+        store_words(0)
 
         y[1] = placed_tile([P, PACK, PAIRS, P], "y1", GATED_BYTES + Y_BYTES)
         copy_sum(nc.scalar.copy, 1, 0)
         copy_sum(nc.vector.tensor_copy, 1, 1, 0)
         copy_sum(nc.scalar.copy, 1, 1, 1)
-        store_values(1, (nc.sync, nc.sync))
+        store_values(1)
         for pair in range(PAIRS):
             round_sum(nc.vector.tensor_copy, 1, pair)
         quantize_sum(1)
-        store_words(1, (nc.sync, nc.sync))
+        store_words(1)
 
         scale_rows = out_2[0].rearrange("(h g r) c -> g r h c", h=HALVES, r=SCALE_ROWS)
         for quad in range(P // QUADRANT):

from contextlib import ExitStack

import concourse.mybir as mybir
from concourse.masks import make_identity

K, T, S, N = 1024, 1024, 512, 512
P = 128
PACK = 4
LIST_ROWS = 16
QUADRANT = 32
SCALE_ROWS = 4
PASSES = K // (P * PACK)
LAYERS = 2
HALVES = 2
HALF = N // HALVES
WORDS = HALF // PACK
BLOCKS = S // P
SIDES = P // WORDS
PAIRS = BLOCKS // SIDES

FLOPS = 2 * 2 * K * N * S
BYTES = 2 * K * N * 4 + K * T + K * T // 32 + 2 * T * 4 + P * (S // 16) * 2 + N * S * 4 + N * S + N * S // 32

F32 = mybir.dt.float32
BF16 = mybir.dt.bfloat16
I32 = mybir.dt.int32
U32 = mybir.dt.uint32
U16 = mybir.dt.uint16
U8 = mybir.dt.uint8
FP8X4 = mybir.dt.float8_e4m3fn_x4
MAX = mybir.AluOpType.max
MULT = mybir.AluOpType.mult
COPY = mybir.ActivationFunctionType.Copy

VECTOR_COLUMNS_FIRST = (128, 176)
VECTOR_COLUMNS = 128
VECTOR_COLUMNS_LAST = 144
GATED_BYTES = PACK * P * 4
Y_BYTES = PAIRS * GATED_BYTES


def tile_picked_zsmoe_relu_po_kernel(
    tc, x_words, x_scales, w1, w2, gate, offs, out_0, out_1, out_2
):
    nc = tc.nc
    weights = (w1, w2)
    steps = [(h, d) for h in range(HALVES) for d in range(LAYERS)]
    pieces = [step + (a,) for step in steps for a in range(PASSES)]

    with ExitStack() as ctx:
        keep = ctx.enter_context(tc.tile_pool(name="keep", bufs=1))
        placed = ctx.enter_context(tc.tile_pool(name="placed", bufs=1))
        psum = ctx.enter_context(tc.psum_pool(name="psum", bufs=1))

        def tile(shape, dtype, name, tag=None):
            return keep.tile(shape, dtype, name=name, tag=tag or name, align_bytes=256)

        def placed_tile(shape, name, offset):
            return placed.tile(shape, F32, name=name, offset=offset, align_bytes=256)

        def bank(name, shape):
            return psum.tile(shape, F32, name=name, tag=name)

        offsets = keep.tile([P, S // LIST_ROWS], U16, name="offsets")
        word_table = [tile([P, T], U32, "word_table%d" % a) for a in range(PASSES)]
        scale_table = tile([P, T], U8, "scale_table")
        gate_table = tile([P, T], F32, "gate_table")
        rounded = {q: tile([P, HALF, PACK], BF16, "rounded%d%d%d" % q) for q in pieces}
        w_words = {q: tile([P, HALF], U32, "w_words%d%d%d" % q) for q in pieces}
        w_scales = {q: tile([P, HALF], U8, "w_scales%d%d%d" % q) for q in pieces}
        picked_first = tile([P, S], U32, "picked_first")
        picked_scales = tile([P, S], U8, "picked_scales")
        picked_gate = tile([P, S], F32, "picked_gate")
        identity = tile([P, P], F32, "identity")
        y_rounded = [tile([P, PAIRS * P, PACK], BF16, "y_rounded%d" % h) for h in range(HALVES)]
        y_words = [tile([P, PAIRS * P], U32, "y_words%d" % h) for h in range(HALVES)]
        y_scales = tile([P, HALVES, PAIRS * P], U8, "y_scales")
        raw, picked_words, products, gated, sums, y = {}, {}, {}, {}, {}, {}

        def load_words(a):
            nc.sync.dma_start(
                out=word_table[a][:].bitcast(I32), in_=x_words[a].rearrange("p c r -> p (c r)").bitcast(I32)
            )

        def load_weights(q):
            h, d, a = q
            rows = weights[d][a * P * PACK : (a + 1) * P * PACK, h * HALF : (h + 1) * HALF]
            if q == pieces[-1]:
                raw[q] = placed_tile([P, PACK, HALF], "raw_last", 0)
            else:
                raw[q] = tile([P, PACK, HALF], F32, "raw%d%d%d" % q)
            nc.sync.dma_start(out=raw[q][:], in_=rows.rearrange("(p j) c -> p j c", j=PACK))

        def interleave(copy, dst, src):
            copy(dst.rearrange("p (c i) j -> p c j i", i=2), src.rearrange("p j (c i) -> p c j i", i=2))

        def round_weights(q, vector_columns=0):
            split = HALF - vector_columns
            interleave(nc.scalar.copy, rounded[q][:, :split, :], raw[q][:, :, :split])
            if vector_columns:
                interleave(nc.vector.tensor_copy, rounded[q][:, split:, :], raw[q][:, :, split:])

        def quantize_weights(q):
            nc.vector.quantize_mx(
                out=w_words[q][:].bitcast(FP8X4),
                scales=w_scales[q][:],
                in_=rounded[q][:].rearrange("p c j -> p (c j)"),
            )

        def multiply(q, pair, opens=None):
            h, d, a = q
            opens = a == 0 if opens is None else opens
            for side in range(SIDES):
                b = PAIRS * side + pair
                if opens:
                    products[h, d, b] = bank("product%d" % b, [P, HALF])
                tokens = slice(b * P, (b + 1) * P)
                nc.tensor.matmul_mx(
                    out=products[h, d, b][:],
                    lhsT=picked_words[a, b].bitcast(FP8X4),
                    lhsT_scale=picked_scales[SCALE_ROWS * a : P, tokens],
                    rhs=w_words[q][:].bitcast(FP8X4),
                    rhs_scale=w_scales[q][:],
                    start=opens,
                    stop=not opens,
                )

        def apply_gate(step, pair, into):
            h, d = step
            gated[h, d, pair] = into
            for side in range(SIDES):
                b = PAIRS * side + pair
                nc.vector.tensor_scalar(
                    out=into[:, :, side, :],
                    in0=products[h, d, b][:].rearrange("p (i t) -> p t i", t=PACK),
                    scalar1=0.0,
                    scalar2=token_gate[:, b, d : d + 1],
                    op0=MAX,
                    op1=MULT,
                )

        def turn(step, pair):
            h, d = step
            if d == 0:
                if (h, pair) == (HALVES - 1, PAIRS - 1):
                    sums[h, pair] = [bank(name, [P, PACK // 2, P]) for name in ("sum3", "sum0")]
                else:
                    sums[h, pair] = [bank("sum%d" % (PAIRS * h + pair), [P, PACK, P])]
            share = PACK // len(sums[h, pair])
            for t in range(PACK):
                nc.tensor.matmul(
                    out=sums[h, pair][t // share][:, t % share, :],
                    lhsT=gated[h, d, pair][:, t, :, :].rearrange("p s i -> p (s i)"),
                    rhs=identity[:],
                    is_transpose=True,
                    start=(d == 0 and t % share == 0),
                    stop=(d == LAYERS - 1 and t % share == share - 1),
                )

        def copy_sum(copy, h, pair, part=0):
            share = PACK // len(sums[h, pair])
            copy(y[h][:, part * share : (part + 1) * share, pair, :], sums[h, pair][part][:])

        def round_sum(copy, h, pair):
            interleave(copy, y_rounded[h][:, pair * P : (pair + 1) * P, :], y[h][:, :, pair, :])

        def quantize_sum(h):
            nc.vector.quantize_mx(
                out=y_words[h][:].bitcast(FP8X4),
                scales=y_scales[:, h, :],
                in_=y_rounded[h][:].rearrange("p c t -> p (c t)"),
            )

        def side_of(side):
            return slice(side * WORDS, (side + 1) * WORDS), slice(side * PAIRS * P, (side + 1) * PAIRS * P)

        def store_values(h):
            rows = out_0[h * HALF : (h + 1) * HALF, :].rearrange("(i t) c -> i t c", t=PACK)
            for side in range(SIDES):
                held, tokens = side_of(side)
                nc.sync.dma_start(out=rows[:, :, tokens], in_=y[h][held].rearrange("p t u j -> p t (u j)"))

        def store_words(h):
            words = out_1[0, h * WORDS : (h + 1) * WORDS].rearrange("i c r -> i (c r)").bitcast(I32)
            for side in range(SIDES):
                held, tokens = side_of(side)
                nc.sync.dma_start(out=words[:, tokens], in_=y_words[h][held].bitcast(I32))

        nc.vector.memset(gate_table[:].bitcast(I32), 0)
        nc.vector.memset(scale_table[:].bitcast(I32), 0)
        nc.any.memset(identity[:], 0.0)
        make_identity(nc, identity[:], nomemset=True)

        load_words(0)
        nc.sync.dma_start(offsets[:], offs)
        nc.sync.dma_start(out=gate_table[0:LAYERS, :], in_=gate[:, 0, :])
        for quad in range(P // QUADRANT):
            nc.sync.dma_start(
                out=scale_table[QUADRANT * quad : QUADRANT * quad + SCALE_ROWS * PASSES, :].bitcast(I32),
                in_=x_scales[:, SCALE_ROWS * quad : SCALE_ROWS * (quad + 1), :].bitcast(I32),
            )
        load_weights(pieces[0])
        load_weights(pieces[1])
        load_words(1)
        for q in pieces[PASSES:]:
            load_weights(q)

        nc.scalar.activation(picked_gate[:], gate_table[:].indirect(offsets[:]), COPY)
        nc.vector.tensor_copy(picked_first[:], word_table[0][:].indirect(offsets[:]))
        for b in range(BLOCKS):
            picked_words[0, b] = picked_first[:, b * P : (b + 1) * P]
        nc.vector.tensor_copy(picked_scales[:], scale_table[:].indirect(offsets[:]))
        turned_gate = bank("sum0", [P, BLOCKS, P])
        for b in range(BLOCKS):
            nc.tensor.transpose(turned_gate[:, b, :], picked_gate[:, b * P : (b + 1) * P], identity[:])
        round_weights(pieces[0], VECTOR_COLUMNS_FIRST[0])
        quantize_weights(pieces[0])
        multiply(pieces[0], 0)
        round_weights(pieces[1], VECTOR_COLUMNS_FIRST[1])
        quantize_weights(pieces[1])
        token_gate = tile([P, BLOCKS, LAYERS], F32, "token_gate", "raw001")
        nc.scalar.copy(token_gate[:], turned_gate[:, :, 0:LAYERS])
        picked_second = tile([P, BLOCKS, P], U32, "picked_second")
        for pair in range(PAIRS):
            for side in range(SIDES):
                b = PAIRS * side + pair
                picked_words[1, b] = picked_second[:, b, :]
                nc.vector.tensor_copy(
                    picked_words[1, b],
                    word_table[1][:].indirect(offsets[:, b * P // LIST_ROWS : (b + 1) * P // LIST_ROWS]),
                )
            multiply(pieces[1], pair, pair == 1)
        multiply(pieces[0], 1, False)

        gated_shape = [P, PACK, SIDES, WORDS]
        for n, step in enumerate(steps):
            apply_gate(step, 0, tile(gated_shape, F32, "gated%d%d0" % step))
            if n > 0:
                turn(steps[n - 1], 1)
            turn(step, 0)
            if step == steps[-1]:
                apply_gate(step, 1, tile(gated_shape, F32, "gated%d%d1" % step))
                turn(step, 1)
                break
            first, second = pieces[PASSES * (n + 1) : PASSES * (n + 2)]
            round_weights(first)
            round_weights(second, VECTOR_COLUMNS_LAST if second == pieces[-1] else VECTOR_COLUMNS)
            for q in (first, second):
                quantize_weights(q)
                multiply(q, 0)
            if second == pieces[-1]:
                apply_gate(step, 1, placed_tile(gated_shape, "gated_on_raw_last", 0))
            else:
                apply_gate(step, 1, tile(gated_shape, F32, "gated%d%d1" % step, "raw%d%d%d" % second))
            multiply(first, 1)
            multiply(second, 1)

        y[0] = placed_tile([P, PACK, PAIRS, P], "y0", GATED_BYTES)
        for pair in range(PAIRS):
            copy_sum(nc.scalar.copy, 0, pair)
        for pair in range(PAIRS):
            round_sum(nc.scalar.copy, 0, pair)
        store_values(0)
        quantize_sum(0)
        store_words(0)

        y[1] = placed_tile([P, PACK, PAIRS, P], "y1", GATED_BYTES + Y_BYTES)
        copy_sum(nc.scalar.copy, 1, 0)
        copy_sum(nc.vector.tensor_copy, 1, 1, 0)
        copy_sum(nc.scalar.copy, 1, 1, 1)
        store_values(1)
        for pair in range(PAIRS):
            round_sum(nc.vector.tensor_copy, 1, pair)
        quantize_sum(1)
        store_words(1)

        scale_rows = out_2[0].rearrange("(h g r) c -> g r h c", h=HALVES, r=SCALE_ROWS)
        for quad in range(P // QUADRANT):
            side, group = divmod(quad, 2)
            queue = nc.scalar if group else nc.sync
            queue.dma_start(
                out=scale_rows[group][:, :, side_of(side)[1]].bitcast(I32),
                in_=y_scales[QUADRANT * quad : QUADRANT * quad + SCALE_ROWS].bitcast(I32),
            )
